import numpy as np
import ml_dtypes


def mxq(x, axis, fmt="e4m3"):
    dtype, down = {"e4m3": (ml_dtypes.float8_e4m3fn, 7), "e5m2": (ml_dtypes.float8_e5m2, 14)}[fmt]
    v = np.moveaxis(np.asarray(x, np.float32).astype(ml_dtypes.bfloat16).astype(np.float64), axis, -1)
    blocks = v.reshape(v.shape[:-1] + (-1, 32))
    amax = np.abs(blocks).max(-1, keepdims=True)
    byte = np.maximum(np.where(amax > 0, np.frexp(amax)[1] - 1 + 127, 0) - down, 1)
    scale = np.exp2(byte - 127.0)
    codes = (blocks / scale).astype(np.float32).astype(dtype).astype(np.float64)
    return np.moveaxis((codes * scale).reshape(v.shape), -1, axis)


WIDE = False


def mx_kscale(k):
    if not WIDE:
        return np.ones(k)
    levels = np.array([10, -10, 5, -5, 0])
    if k % 512:
        return np.exp2(np.random.permutation(np.resize(levels, k // 32))).repeat(32)
    a = np.empty((k // 512, 16))
    for p in range(k // 512):
        a[p, :8] = np.random.permutation(np.resize(levels, 8))
        for g in range(8):
            far = levels[np.abs(levels - a[p, g]) >= 10]
            a[p, g + 8] = far[np.random.randint(len(far))]
    return np.exp2(a.ravel()).repeat(32)


BF16 = ml_dtypes.bfloat16


def bf(x):
    return np.asarray(x, np.float32).astype(BF16)


def f64(x):
    return np.asarray(x).astype(np.float64)


T, HEADS, D, V = 512, 4, 1024, 1024


def setup_inputs():
    s = mx_kscale(D)
    u = mx_kscale(HEADS * T)
    x = np.random.standard_normal((T, D)) * s
    r = np.random.standard_normal((T, D))
    w = np.random.standard_normal((D, HEADS * D)) / np.sqrt(D) / s[:, None]
    c = np.random.uniform(0.5, 1.5, HEADS * T) * u
    g = np.random.standard_normal((HEADS * T, V)) / np.sqrt(HEADS * T) / u[:, None]
    return {"x": bf(x),
            "r": bf(r),
            "w": bf(w),
            "c": bf(c.reshape(HEADS, T)),
            "g": bf(g)}


def reference(x, r, w, c, g):
    z = mxq(f64(x), 1, "e4m3") @ mxq(f64(w), 0, "e4m3")
    z = z.reshape(T, HEADS, D).transpose(1, 0, 2)
    h = (z / (1.0 + np.exp(-z)) + f64(r)) * f64(c).reshape(HEADS, T, 1)
    h = h.reshape(HEADS * T, D)
    du = mxq(h, 0, "e4m3").T @ mxq(f64(g), 0, "e4m3")
    return du

@@ -1,0 +1,368 @@
+from contextlib import ExitStack
+
+import concourse.mybir as mybir
+from concourse.masks import make_identity
+
+T, HEADS, D, V = 512, 4, 1024, 1024
+FLOPS = 2 * T * D * HEADS * D + 2 * HEADS * T * D * V
+
+F32 = mybir.dt.float32
+BF16 = mybir.dt.bfloat16
+U32 = mybir.dt.uint32
+U8 = mybir.dt.uint8
+FP8X4 = mybir.dt.float8_e4m3fn_x4
+ADD = mybir.AluOpType.add
+MULT = mybir.AluOpType.mult
+SILU = mybir.ActivationFunctionType.Silu
+
+P = 128
+PACK = 4
+BANK = 512
+PAIR = 256
+GROUPS = ([[(j, 2 * dp), (j, 2 * dp + 1)] for j in range(HEADS) for dp in (0, 1)]
+          + [[(j, 4), (j, 5)] for j in range(HEADS)] + [[(j, 6), (j, 7)] for j in (0, 1)]
+          + [[(2, dt), (3, dt)] for dt in (6, 7)])
+TURNED = (0, 1, 2, 3, 4, 5, 6, 7, 14, 15)
+LOADS = "x0 x1 w000 w001 r0 c g0 w100 w101 g1 w200 w201 g2 w300 w301 g3 r1 w010 w011 w110 w111"
+W_SHARE = [256] * 10 + [208] * 4 + [256] * 2
+G_SHARE = 272
+W_RAW_TILES = 6
+OUT_TILES = 8
+
+
+def tile_medusa_unembedding_grad_s7_kernel(tc, x, r, w, c, g, out):
+    nc = tc.nc
+    with ExitStack() as ctx:
+        sb = ctx.enter_context(tc.tile_pool(name="sb", bufs=1))
+        ps = ctx.enter_context(tc.psum_pool(name="ps", bufs=1))
+
+        def tiles(name, count, shape, dtype):
+            return [sb.tile(shape, dtype, name="%s%d" % (name, i), align_bytes=64) for i in range(count)]
+
+        banks = [ps.tile([P, BANK], F32, name="bank%d" % i) for i in range(8)]
+        ident32 = sb.tile([P, P], F32, name="ident32", align_bytes=64)
+        ident16 = sb.tile([P, P], BF16, name="ident16", align_bytes=64)
+        warm = sb.tile([P, 2], F32, name="warm", align_bytes=64)
+        x_raw = tiles("x_raw", 2, [P, 2, D], BF16)
+        r_raw = tiles("r_raw", 2, [P, PACK, BANK], BF16)
+        c_tok = sb.tile([P, HEADS, 16], BF16, name="c_tok", align_bytes=64)
+        w_raw = [tiles("w_raw%d_" % i, 2, [P, PACK, BANK], BF16) for i in range(W_RAW_TILES)]
+        g_raw = tiles("g_raw", HEADS, [P, PACK, V], BF16)
+        x_grp = sb.tile([P, 2, T, PACK], BF16, name="x_grp", align_bytes=64)
+        w_grp = tiles("w_grp", 3, [P, 2, PAIR, PACK], BF16)
+        g_grp = tiles("g_grp", 2, [P, BANK, PACK], BF16)
+        x_codes = tiles("x_codes", 2, [P, T], U32)
+        x_scales = tiles("x_scales", 2, [P, T], U8)
+        w_codes = tiles("w_codes", 3, [P, 2, PAIR], U32)
+        w_scales = tiles("w_scales", 3, [P, 2, PAIR], U8)
+        g_codes = tiles("g_codes", 8, [P, BANK], U32)
+        g_scales = tiles("g_scales", 8, [P, BANK], U8)
+        h_codes = tiles("h_codes", 16, [P, PAIR], U32)
+        h_scales = tiles("h_scales", 16, [P, PAIR], U8)
+        silu = tiles("silu", 4, [P, BANK], F32)
+        silu2 = tiles("silu2_", 2, [P, 2, PAIR, 2], F32)
+        h_grp = tiles("h_grp", 2, [P, PAIR, PACK], BF16)
+        r_turned = tiles("r_turned", 2, [P, 2, T], F32)
+        du = tiles("du", OUT_TILES, [P, BANK], F32)
+
+        def interleave(copy, dst, src):
+            copy(out=dst.rearrange("p (c i) t -> p c t i", i=4), in_=src.rearrange("p t (c i) -> p c t i", i=4))
+
+        def quantize(codes, scales, grouped):
+            nc.vector.quantize_mx(out=codes.bitcast(FP8X4), scales=scales, in_=grouped)
+
+        def mx(acc, lhs_codes, lhs_scales, rhs_codes, rhs_scales, start, stop):
+            nc.tensor.matmul_mx(out=acc, lhsT=lhs_codes.bitcast(FP8X4), lhsT_scale=lhs_scales,
+                                rhs=rhs_codes.bitcast(FP8X4), rhs_scale=rhs_scales, start=start, stop=stop)
+
+        def raw_w(j, half):
+            return w_raw[(half * HEADS + j) % W_RAW_TILES]
+
+        def load_w(j, half, k):
+            cols = slice(j * D + half * BANK, j * D + (half + 1) * BANK)
+            nc.sync.dma_start(out=raw_w(j, half)[k][:], in_=w[k * 512:(k + 1) * 512, cols].rearrange("(p t) n -> p t n", t=PACK))
+
+        def load_g(j):
+            nc.sync.dma_start(out=g_raw[j][:], in_=g[j * T:(j + 1) * T, :].rearrange("(p t) n -> p t n", t=PACK))
+
+        def load_x(a):
+            nc.sync.dma_start(out=x_raw[a][:], in_=x.rearrange("(p t) n -> p t n", t=PACK)[:, 2 * a:2 * a + 2, :])
+
+        def load_r(half):
+            nc.sync.dma_start(out=r_raw[half][:], in_=r[:, half * BANK:(half + 1) * BANK].rearrange("(p t) n -> p t n", t=PACK))
+
+        def turned(i):
+            return i in TURNED
+
+        def w_interleave(copy, i, k, lo, hi):
+            (j0, dt0), (j1, dt1) = GROUPS[i]
+            cuts = [lo, hi] if j0 == j1 or hi <= P or lo >= P else [lo, P, hi]
+            for a, b in zip(cuts, cuts[1:]):
+                j, dt = GROUPS[i][a // P]
+                base = dt % 4 * P - a // P * P
+                interleave(copy, w_grp[i % 3][:, k, a:b, :], raw_w(j, dt // 4)[k][:, :, base + a:base + b])
+
+        def w_interleave_vector(i):
+            w_interleave(nc.vector.tensor_copy, i, 0, 0, W_SHARE[i])
+
+        def w_interleave_scalar(i):
+            if W_SHARE[i] < PAIR:
+                w_interleave(nc.scalar.copy, i, 0, W_SHARE[i], PAIR)
+            w_interleave(nc.scalar.copy, i, 1, 0, PAIR)
+
+        def w_quantize(i):
+            quantize(w_codes[i % 3][:].rearrange("p k n -> p (k n)"), w_scales[i % 3][:].rearrange("p k n -> p (k n)"),
+                     w_grp[i % 3][:].rearrange("p k n t -> p (k n t)"))
+
+        def g_interleave_vector(i):
+            j, vh = divmod(i, 2)
+            interleave(nc.vector.tensor_copy, g_grp[i % 2][:, 0:G_SHARE, :], g_raw[j][:, :, vh * BANK:vh * BANK + G_SHARE])
+
+        def g_interleave_scalar(i):
+            j, vh = divmod(i, 2)
+            interleave(nc.scalar.copy, g_grp[i % 2][:, G_SHARE:BANK, :], g_raw[j][:, :, vh * BANK + G_SHARE:(vh + 1) * BANK])
+
+        def g_quantize(i):
+            j, vh = divmod(i, 2)
+            quantize(g_codes[2 * j + vh][:], g_scales[2 * j + vh][:], g_grp[i % 2][:].rearrange("p n t -> p (n t)"))
+
+        def x_transpose(t):
+            words = x_raw[t // 2][:, t % 2, :].bitcast(F32)
+            for k in range(2):
+                for u in range(2):
+                    q = 2 * k + u
+                    nc.tensor.transpose(banks[4 + t][:, q * P:(q + 1) * P], words[:, 256 * k + u:256 * (k + 1):2], ident32[:])
+
+        def x_copy(copy, t):
+            dst = x_grp[:, :, t * P:(t + 1) * P, :].rearrange("p k m t -> p k (m t)").bitcast(F32).rearrange("p k (m u) -> p k m u", u=2)
+            copy(out=dst, in_=banks[4 + t][:].rearrange("p (k u m) -> p k m u", k=2, u=2))
+
+        def x_quantize(k):
+            quantize(x_codes[k][:], x_scales[k][:], x_grp[:, k, :, :].rearrange("p n t -> p (n t)"))
+
+        def r_transpose(dp, bank):
+            view = bank[:].bitcast(BF16)
+            for a in range(2):
+                for t in range(PACK):
+                    q = a * PACK + t
+                    col = (dp % 2) * PAIR + a * P
+                    nc.tensor.transpose(view[:, q * P:(q + 1) * P], r_raw[dp // 2][:, t, col:col + P], ident16[:])
+
+        def r_copy(dp, bank):
+            nc.scalar.copy(out=r_turned[dp % 2][:].rearrange("p a n -> p (a n)"), in_=bank[:].bitcast(BF16))
+
+        def project(i, a):
+            for t in ((None,) if turned(i) else (2 * a, 2 * a + 1)):
+                for k in range(2):
+                    if turned(i):
+                        cols = slice(a * P, (a + 1) * P)
+                        mx(banks[a][:], w_codes[i % 3][:, k, cols], w_scales[i % 3][:, k, cols],
+                           x_codes[k][:], x_scales[k][:], k == 0, k == 1)
+                    else:
+                        cols = slice(t * P, (t + 1) * P)
+                        mx(banks[a][:, t % 2 * PAIR:(t % 2 + 1) * PAIR], x_codes[k][:, cols], x_scales[k][:, cols],
+                           w_codes[i % 3][:, k, :], w_scales[i % 3][:, k, :], k == 0, k == 1)
+
+        def activate(i, a):
+            if turned(i):
+                nc.scalar.activation(out=silu[(2 * i + a) % 4][:], in_=banks[a][:], func=SILU)
+            else:
+                nc.scalar.activation(out=silu2[i % 2][:, a, :, :], in_=banks[a][:].rearrange("p (e n) -> p n e", e=2), func=SILU)
+
+        def turn_bank(i, a):
+            return banks[2 + a]
+
+        def turn(i, a):
+            dt = GROUPS[i][a][1]
+            for t in range(PACK):
+                cols = slice(t * P, (t + 1) * P)
+                acc = turn_bank(i, a)[:, cols]
+                nc.tensor.matmul(acc, lhsT=r_turned[dt // 2 % 2][:, dt % 2, cols], rhs=ident32[:], start=True, stop=False, is_transpose=True)
+                nc.tensor.matmul(acc, lhsT=silu[(2 * i + a) % 4][:, cols], rhs=ident32[:], start=False, stop=True, is_transpose=True)
+
+        def c_spread(i, a, n):
+            return c_tok[:, GROUPS[i][a][0], 0:PACK].unsqueeze(1).to_broadcast([P, n, PACK])
+
+        def weigh_turned(i, a):
+            nc.vector.tensor_tensor(out=h_grp[i % 2][:, a * P:(a + 1) * P, :], in0=turn_bank(i, a)[:].rearrange("p (t n) -> p n t", t=PACK),
+                                    in1=c_spread(i, a, P), op=MULT)
+
+        def add_direct(i, lo, hi):
+            base = GROUPS[i][0][1] % 4 * P
+            nc.vector.tensor_tensor(out=silu2[i % 2][:, :, lo:hi, :], in0=silu2[i % 2][:, :, lo:hi, :],
+                                    in1=r_raw[1][:, :, base + lo:base + hi].rearrange("p (a e) n -> p a n e", e=2), op=ADD)
+
+        def weigh_direct(i, lo, hi):
+            nc.vector.tensor_tensor(out=h_grp[i % 2][:, lo:hi, :].rearrange("p n (a e) -> p n a e", e=2),
+                                    in0=silu2[i % 2][:, :, lo:hi, :].rearrange("p a n e -> p n a e"),
+                                    in1=c_spread(i, 0, hi - lo).rearrange("p n (a e) -> p n a e", e=2), op=MULT)
+
+        def h_quantize(i, lo, hi):
+            quantize(h_codes[i][:, lo:hi], h_scales[i][:, lo:hi], h_grp[i % 2][:, lo:hi, :].rearrange("p n t -> p (n t)"))
+
+        def grad_pass(bank, dt, vh, j):
+            i, a = [(m, units.index((j, dt))) for m, units in enumerate(GROUPS) if (j, dt) in units][0]
+            cols = slice(a * P, (a + 1) * P)
+            mx(bank[:], h_codes[i][:, cols], h_scales[i][:, cols], g_codes[2 * j + vh][:], g_scales[2 * j + vh][:],
+               j == 0, j == HEADS - 1)
+
+        stored = []
+
+        def grad_out(copy, bank, dt, vh):
+            stage = du[len(stored) % OUT_TILES]
+            stored.append((dt, vh))
+            copy(out=stage[:], in_=bank[:])
+            nc.sync.dma_start(out=out[dt * P:(dt + 1) * P, vh * BANK:(vh + 1) * BANK], in_=stage[:])
+
+        bank_of = {(0, 0): 4, (0, 1): 5, (1, 0): 6, (1, 1): 7, (2, 0): 2, (3, 0): 3, (2, 1): 4, (3, 1): 6,
+                   (4, 0): 5, (4, 1): 7, (5, 0): 2, (5, 1): 3, (6, 0): 4, (6, 1): 6, (7, 0): 5, (7, 1): 7}
+        passes = {i: [(dt, i % 2, i // 2 - 1) for dt in (0, 1)] for i in range(2, 10)}
+        passes[9] = passes[9] + [(dt, 0, j) for dt in (2, 3) for j in range(HEADS)]
+        passes[10] = [(dt, 1, j) for dt in (2, 3) for j in range(HEADS)]
+        passes[11] = [(4, vh, j) for j in (0, 1) for vh in (0, 1)]
+        passes[12] = [(5, vh, j) for j in (0, 1) for vh in (0, 1)] + [(dt, vh, 2) for dt in (4, 5) for vh in (0, 1)]
+        passes[13] = [(dt, vh, 3) for dt in (5, 4) for vh in (0, 1)]
+        passes[14] = [(6, vh, 0) for vh in (0, 1)]
+        passes[15] = [(6, vh, 1) for vh in (0, 1)] + [(7, vh, j) for j in (0, 1) for vh in (0, 1)]
+        outs = {9: [(0, 0), (1, 0)], 10: [(0, 1), (1, 1)], 11: [(2, 0), (3, 0)], 12: [(2, 1), (3, 1)],
+                13: [(5, 0), (5, 1)], 14: [(4, 0), (4, 1)]}
+
+        ctx.enter_context(tc.manual_schedule(engines={mybir.EngineType.SP}))
+
+        for name in LOADS.split():
+            if name[0] == "x":
+                load_x(int(name[1]))
+            if name[0] == "r":
+                load_r(int(name[1]))
+            if name[0] == "g":
+                load_g(int(name[1]))
+            if name[0] == "w":
+                load_w(int(name[1]), int(name[2]), int(name[3]))
+            if name[0] == "c":
+                nc.sync.dma_start(out=c_tok[:, :, 0:PACK], in_=c.rearrange("j (p t) -> p j t", t=PACK))
+
+        make_identity(nc, ident32[:])
+        make_identity(nc, ident16[:])
+        nc.vector.memset(warm[:], 0.0)
+        nc.scalar.activation(out=warm[:, 1:2], in_=warm[:, 0:1], func=SILU)
+
+        for t in range(PACK):
+            x_transpose(t)
+        w_interleave_vector(0)
+        x_copy(nc.scalar.copy, 0)
+        w_interleave_vector(1)
+        x_copy(nc.scalar.copy, 1)
+        w_interleave_scalar(0)
+        x_copy(nc.vector.tensor_copy, 2)
+        x_copy(nc.vector.tensor_copy, 3)
+        w_interleave_scalar(1)
+        w_quantize(0)
+        x_quantize(0)
+        x_quantize(1)
+        r_transpose(0, banks[2])
+        r_transpose(1, banks[3])
+        r_copy(0, banks[2])
+        project(0, 0)
+        project(0, 1)
+        w_quantize(1)
+
+        n = len(GROUPS)
+        w_at = {i: [i + 2] for i in range(2, n - 2)}
+        w_at[1] = [2, 3]
+        g_at = {i: [i] for i in range(2, 8)}
+        g_at[0] = [0, 1]
+        for i in range(n):
+            prev = i >= 1
+            ws = w_at.get(i, [])
+            gs = g_at.get(i, [])
+            if i in (2, 4):
+                load_w(i // 2 + 1, 1, 0)
+                load_w(i // 2 + 1, 1, 1)
+            if i == 0:
+                g_interleave_scalar(0)
+            activate(i, 0)
+            activate(i, 1)
+            if i == 0:
+                r_copy(1, banks[3])
+            for dt, vh in outs.get(i, []):
+                if i != 13:
+                    grad_out(nc.scalar.copy, banks[bank_of[dt, vh]], dt, vh)
+            for dt, vh, j in passes.get(i, []):
+                grad_pass(banks[bank_of[dt, vh]], dt, vh, j)
+            for m in ws:
+                w_interleave_scalar(m)
+            for m in gs:
+                if m:
+                    g_interleave_scalar(m)
+            for dt, vh in outs.get(i, []):
+                if i == 13:
+                    grad_out(nc.scalar.copy, banks[bank_of[dt, vh]], dt, vh)
+            if i == 0:
+                g_interleave_vector(0)
+                g_interleave_vector(1)
+                g_quantize(0)
+            elif i == 1:
+                w_interleave_vector(2)
+                weigh_turned(0, 0)
+                w_interleave_vector(3)
+                weigh_turned(0, 1)
+                w_quantize(2)
+                h_quantize(0, 0, PAIR)
+                g_quantize(1)
+                w_quantize(3)
+            elif turned(i - 1):
+                weigh_turned(i - 1, 0)
+                if 3 <= i <= 8:
+                    g_quantize(i - 1)
+                for m in ws:
+                    w_interleave_vector(m)
+                weigh_turned(i - 1, 1)
+                for m in gs:
+                    g_interleave_vector(m)
+                if i == n - 1:
+                    h_quantize(i - 1, 0, P)
+                    h_quantize(i - 1, P, PAIR)
+                elif gs:
+                    h_quantize(i - 1, 0, PAIR)
+                    w_quantize(i + 2)
+                else:
+                    w_quantize(i + 2)
+                    h_quantize(i - 1, 0, PAIR)
+            elif ws:
+                add_direct(i - 1, 0, PAIR)
+                w_interleave_vector(i + 2)
+                weigh_direct(i - 1, 0, PAIR)
+                w_quantize(i + 2)
+                h_quantize(i - 1, 0, PAIR)
+            else:
+                for a in range(2):
+                    add_direct(i - 1, a * P, (a + 1) * P)
+                for a in range(2):
+                    weigh_direct(i - 1, a * P, (a + 1) * P)
+                for a in range(2):
+                    h_quantize(i - 1, a * P, (a + 1) * P)
+            if i + 1 < n:
+                project(i + 1, 0)
+                project(i + 1, 1)
+            if turned(i):
+                turn(i, 0)
+                turn(i, 1)
+            if i == 8:
+                r_transpose(3, banks[3])
+                r_copy(3, banks[3])
+
+        last = n - 1
+        for j in (2, 3):
+            for vh in range(2):
+                grad_pass(banks[bank_of[6, vh]], 6, vh, j)
+        for vh in range(2):
+            grad_out(nc.scalar.copy, banks[bank_of[6, vh]], 6, vh)
+        weigh_turned(last, 0)
+        weigh_turned(last, 1)
+        for a in range(2):
+            h_quantize(last, a * P, (a + 1) * P)
+        for j in (2, 3):
+            for vh in range(2):
+                grad_pass(banks[bank_of[7, vh]], 7, vh, j)
+        grad_out(nc.scalar.copy, banks[bank_of[7, 0]], 7, 0)
+        grad_out(nc.vector.tensor_copy, banks[bank_of[7, 1]], 7, 1)

@@ -22,11 +22,14 @@ PAIR = 256
 GROUPS = ([[(j, 2 * dp), (j, 2 * dp + 1)] for j in range(HEADS) for dp in (0, 1)]
           + [[(j, 4), (j, 5)] for j in range(HEADS)] + [[(j, 6), (j, 7)] for j in (0, 1)]
           + [[(2, dt), (3, dt)] for dt in (6, 7)])
-TURNED = (0, 1, 2, 3, 4, 5, 6, 7, 14, 15)
-LOADS = "x0 x1 w000 w001 r0 c g0 w100 w101 g1 w200 w201 g2 w300 w301 g3 r1 w010 w011 w110 w111"
-W_SHARE = [256] * 10 + [208] * 4 + [256] * 2
-G_SHARE = 272
+TURNED = (0, 1, 2, 3, 4, 5, 6, 7)
+LOADS = "x0 x1 w000 w001 r0 c w100 w101 g0 w200 w201 g1 w300 w301 g2 g3 r1 w010 w011 w110 w111"
+W_SHARE = [512, 256, 512] + [256] * 7 + [208] * 4 + [128] * 2
+G_SHARE = [208] * 8
 W_RAW_TILES = 6
+SPLIT = 14
+RC_FIRST = False
+RC_S = True
 OUT_TILES = 8
 
 
@@ -60,7 +63,7 @@ def tile_medusa_unembedding_grad_s7_kernel(tc, x, r, w, c, g, out):
         h_codes = tiles("h_codes", 16, [P, PAIR], U32)
         h_scales = tiles("h_scales", 16, [P, PAIR], U8)
         silu = tiles("silu", 4, [P, BANK], F32)
-        silu2 = tiles("silu2_", 2, [P, 2, PAIR, 2], F32)
+        silu2 = tiles("silu2_", 3, [P, 2 * BANK], F32)
         h_grp = tiles("h_grp", 2, [P, PAIR, PACK], BF16)
         r_turned = tiles("r_turned", 2, [P, 2, T], F32)
         du = tiles("du", OUT_TILES, [P, BANK], F32)
@@ -103,12 +106,16 @@ def tile_medusa_unembedding_grad_s7_kernel(tc, x, r, w, c, g, out):
                 interleave(copy, w_grp[i % 3][:, k, a:b, :], raw_w(j, dt // 4)[k][:, :, base + a:base + b])
 
         def w_interleave_vector(i):
-            w_interleave(nc.vector.tensor_copy, i, 0, 0, W_SHARE[i])
+            if W_SHARE[i]:
+                w_interleave(nc.vector.tensor_copy, i, 0, 0, min(W_SHARE[i], PAIR))
+            if W_SHARE[i] > PAIR:
+                w_interleave(nc.vector.tensor_copy, i, 1, 0, W_SHARE[i] - PAIR)
 
         def w_interleave_scalar(i):
             if W_SHARE[i] < PAIR:
                 w_interleave(nc.scalar.copy, i, 0, W_SHARE[i], PAIR)
-            w_interleave(nc.scalar.copy, i, 1, 0, PAIR)
+            if W_SHARE[i] < 2 * PAIR:
+                w_interleave(nc.scalar.copy, i, 1, max(W_SHARE[i] - PAIR, 0), PAIR)
 
         def w_quantize(i):
             quantize(w_codes[i % 3][:].rearrange("p k n -> p (k n)"), w_scales[i % 3][:].rearrange("p k n -> p (k n)"),
@@ -116,11 +123,12 @@ def tile_medusa_unembedding_grad_s7_kernel(tc, x, r, w, c, g, out):
 
         def g_interleave_vector(i):
             j, vh = divmod(i, 2)
-            interleave(nc.vector.tensor_copy, g_grp[i % 2][:, 0:G_SHARE, :], g_raw[j][:, :, vh * BANK:vh * BANK + G_SHARE])
+            interleave(nc.vector.tensor_copy, g_grp[i % 2][:, 0:G_SHARE[i], :], g_raw[j][:, :, vh * BANK:vh * BANK + G_SHARE[i]])
 
         def g_interleave_scalar(i):
             j, vh = divmod(i, 2)
-            interleave(nc.scalar.copy, g_grp[i % 2][:, G_SHARE:BANK, :], g_raw[j][:, :, vh * BANK + G_SHARE:(vh + 1) * BANK])
+            if G_SHARE[i] < BANK:
+                interleave(nc.scalar.copy, g_grp[i % 2][:, G_SHARE[i]:BANK, :], g_raw[j][:, :, vh * BANK + G_SHARE[i]:(vh + 1) * BANK])
 
         def g_quantize(i):
             j, vh = divmod(i, 2)
@@ -148,8 +156,8 @@ def tile_medusa_unembedding_grad_s7_kernel(tc, x, r, w, c, g, out):
                     col = (dp % 2) * PAIR + a * P
                     nc.tensor.transpose(view[:, q * P:(q + 1) * P], r_raw[dp // 2][:, t, col:col + P], ident16[:])
 
-        def r_copy(dp, bank):
-            nc.scalar.copy(out=r_turned[dp % 2][:].rearrange("p a n -> p (a n)"), in_=bank[:].bitcast(BF16))
+        def r_copy(copy, dp, bank):
+            copy(out=r_turned[dp % 2][:].rearrange("p a n -> p (a n)"), in_=bank[:].bitcast(BF16))
 
         def project(i, a):
             for t in ((None,) if turned(i) else (2 * a, 2 * a + 1)):
@@ -167,7 +175,9 @@ def tile_medusa_unembedding_grad_s7_kernel(tc, x, r, w, c, g, out):
             if turned(i):
                 nc.scalar.activation(out=silu[(2 * i + a) % 4][:], in_=banks[a][:], func=SILU)
             else:
-                nc.scalar.activation(out=silu2[i % 2][:, a, :, :], in_=banks[a][:].rearrange("p (e n) -> p n e", e=2), func=SILU)
+                parts = 2 if i >= SPLIT else 1
+                nc.scalar.activation(out=silu2[i % 3][:].rearrange("p (b a n e) -> p b a n e", b=parts, a=2, e=2)[:, :, a, :, :],
+                                     in_=banks[a][:].rearrange("p (e b n) -> p b n e", e=2, b=parts), func=SILU)
 
         def turn_bank(i, a):
             return banks[2 + a]
@@ -187,15 +197,18 @@ def tile_medusa_unembedding_grad_s7_kernel(tc, x, r, w, c, g, out):
             nc.vector.tensor_tensor(out=h_grp[i % 2][:, a * P:(a + 1) * P, :], in0=turn_bank(i, a)[:].rearrange("p (t n) -> p n t", t=PACK),
                                     in1=c_spread(i, a, P), op=MULT)
 
+        def silu_part(i, lo, hi):
+            return silu2[i % 3][:, lo * PACK:hi * PACK].rearrange("p (a n e) -> p a n e", a=2, e=2)
+
         def add_direct(i, lo, hi):
-            base = GROUPS[i][0][1] % 4 * P
-            nc.vector.tensor_tensor(out=silu2[i % 2][:, :, lo:hi, :], in0=silu2[i % 2][:, :, lo:hi, :],
+            base = GROUPS[i][lo // P][1] % 4 * P - lo // P * P
+            nc.vector.tensor_tensor(out=silu_part(i, lo, hi), in0=silu_part(i, lo, hi),
                                     in1=r_raw[1][:, :, base + lo:base + hi].rearrange("p (a e) n -> p a n e", e=2), op=ADD)
 
         def weigh_direct(i, lo, hi):
             nc.vector.tensor_tensor(out=h_grp[i % 2][:, lo:hi, :].rearrange("p n (a e) -> p n a e", e=2),
-                                    in0=silu2[i % 2][:, :, lo:hi, :].rearrange("p a n e -> p n a e"),
-                                    in1=c_spread(i, 0, hi - lo).rearrange("p n (a e) -> p n a e", e=2), op=MULT)
+                                    in0=silu_part(i, lo, hi).rearrange("p a n e -> p n a e"),
+                                    in1=c_spread(i, lo // P, hi - lo).rearrange("p n (a e) -> p n a e", e=2), op=MULT)
 
         def h_quantize(i, lo, hi):
             quantize(h_codes[i][:, lo:hi], h_scales[i][:, lo:hi], h_grp[i % 2][:, lo:hi, :].rearrange("p n t -> p (n t)"))
@@ -214,20 +227,26 @@ def tile_medusa_unembedding_grad_s7_kernel(tc, x, r, w, c, g, out):
             copy(out=stage[:], in_=bank[:])
             nc.sync.dma_start(out=out[dt * P:(dt + 1) * P, vh * BANK:(vh + 1) * BANK], in_=stage[:])
 
+        def emit_passes(todo):
+            for dt, vh, j in todo:
+                grad_pass(banks[bank_of[dt, vh]], dt, vh, j)
+
+        def emit_out(todo):
+            for dt, vh in todo:
+                grad_out(nc.scalar.copy, banks[bank_of[dt, vh]], dt, vh)
+
         bank_of = {(0, 0): 4, (0, 1): 5, (1, 0): 6, (1, 1): 7, (2, 0): 2, (3, 0): 3, (2, 1): 4, (3, 1): 6,
-                   (4, 0): 5, (4, 1): 7, (5, 0): 2, (5, 1): 3, (6, 0): 4, (6, 1): 6, (7, 0): 5, (7, 1): 7}
-        passes = {i: [(dt, i % 2, i // 2 - 1) for dt in (0, 1)] for i in range(2, 10)}
+                   (4, 0): 5, (4, 1): 7, (5, 0): 2, (5, 1): 3, (6, 0): 4, (6, 1): 6, (7, 0): 2, (7, 1): 3}
+        passes = {i: [(dt, (i - 3) % 2, (i - 3) // 2) for dt in (0, 1)] for i in range(3, 11)}
         passes[9] = passes[9] + [(dt, 0, j) for dt in (2, 3) for j in range(HEADS)]
-        passes[10] = [(dt, 1, j) for dt in (2, 3) for j in range(HEADS)]
-        passes[11] = [(4, vh, j) for j in (0, 1) for vh in (0, 1)]
+        passes[10] = passes[10] + [(2, 1, j) for j in range(HEADS)]
+        passes[11] = [(3, 1, j) for j in range(HEADS)] + [(4, vh, j) for j in (0, 1) for vh in (0, 1)]
         passes[12] = [(5, vh, j) for j in (0, 1) for vh in (0, 1)] + [(dt, vh, 2) for dt in (4, 5) for vh in (0, 1)]
         passes[13] = [(dt, vh, 3) for dt in (5, 4) for vh in (0, 1)]
         passes[14] = [(6, vh, 0) for vh in (0, 1)]
-        passes[15] = [(6, vh, 1) for vh in (0, 1)] + [(7, vh, j) for j in (0, 1) for vh in (0, 1)]
-        outs = {9: [(0, 0), (1, 0)], 10: [(0, 1), (1, 1)], 11: [(2, 0), (3, 0)], 12: [(2, 1), (3, 1)],
-                13: [(5, 0), (5, 1)], 14: [(4, 0), (4, 1)]}
+        outs = {10: [(0, 0), (1, 0)], 11: [(0, 1), (1, 1)], 12: [(2, 0), (3, 0)], 13: [(2, 1)], 14: [(3, 1)]}
 
-        ctx.enter_context(tc.manual_schedule(engines={mybir.EngineType.SP}))
+        ctx.enter_context(tc.manual_schedule())
 
         for name in LOADS.split():
             if name[0] == "x":
@@ -248,121 +267,93 @@ def tile_medusa_unembedding_grad_s7_kernel(tc, x, r, w, c, g, out):
 
         for t in range(PACK):
             x_transpose(t)
-        w_interleave_vector(0)
-        x_copy(nc.scalar.copy, 0)
-        w_interleave_vector(1)
-        x_copy(nc.scalar.copy, 1)
-        w_interleave_scalar(0)
-        x_copy(nc.vector.tensor_copy, 2)
-        x_copy(nc.vector.tensor_copy, 3)
-        w_interleave_scalar(1)
-        w_quantize(0)
-        x_quantize(0)
-        x_quantize(1)
+        for t in range(PACK):
+            x_copy(nc.scalar.copy, t)
         r_transpose(0, banks[2])
         r_transpose(1, banks[3])
-        r_copy(0, banks[2])
+        w_interleave_vector(0)
+        w_interleave_vector(1)
+        if RC_FIRST:
+            r_copy(nc.scalar.copy, 0, banks[2])
+        w_interleave_scalar(0)
+        w_interleave_scalar(1)
+        x_quantize(0)
+        w_quantize(0)
+        x_quantize(1)
         project(0, 0)
         project(0, 1)
+        if not RC_FIRST:
+            r_copy(nc.scalar.copy, 0, banks[2])
         w_quantize(1)
+        r_copy(nc.scalar.copy if RC_S else nc.vector.tensor_copy, 1, banks[3])
+        activate(0, 0)
+        activate(0, 1)
+        w_interleave_vector(2)
+        w_interleave_scalar(2)
+        project(1, 0)
+        project(1, 1)
+        turn(0, 0)
+        turn(0, 1)
 
         n = len(GROUPS)
-        w_at = {i: [i + 2] for i in range(2, n - 2)}
-        w_at[1] = [2, 3]
-        g_at = {i: [i] for i in range(2, 8)}
-        g_at[0] = [0, 1]
-        for i in range(n):
-            prev = i >= 1
-            ws = w_at.get(i, [])
-            gs = g_at.get(i, [])
+        for i in range(1, n - 1):
             if i in (2, 4):
                 load_w(i // 2 + 1, 1, 0)
                 load_w(i // 2 + 1, 1, 1)
-            if i == 0:
-                g_interleave_scalar(0)
             activate(i, 0)
             activate(i, 1)
-            if i == 0:
-                r_copy(1, banks[3])
-            for dt, vh in outs.get(i, []):
-                if i != 13:
-                    grad_out(nc.scalar.copy, banks[bank_of[dt, vh]], dt, vh)
-            for dt, vh, j in passes.get(i, []):
-                grad_pass(banks[bank_of[dt, vh]], dt, vh, j)
-            for m in ws:
-                w_interleave_scalar(m)
-            for m in gs:
-                if m:
-                    g_interleave_scalar(m)
-            for dt, vh in outs.get(i, []):
-                if i == 13:
-                    grad_out(nc.scalar.copy, banks[bank_of[dt, vh]], dt, vh)
-            if i == 0:
-                g_interleave_vector(0)
-                g_interleave_vector(1)
-                g_quantize(0)
-            elif i == 1:
-                w_interleave_vector(2)
-                weigh_turned(0, 0)
-                w_interleave_vector(3)
-                weigh_turned(0, 1)
-                w_quantize(2)
-                h_quantize(0, 0, PAIR)
-                g_quantize(1)
-                w_quantize(3)
-            elif turned(i - 1):
+            emit_out(outs.get(i, []))
+            if i + 2 < n:
+                w_interleave_scalar(i + 2)
+            if i <= 8:
+                g_interleave_scalar(i - 1)
+            w_quantize(i + 1)
+            if turned(i - 1):
+                w_interleave_vector(i + 2)
                 weigh_turned(i - 1, 0)
-                if 3 <= i <= 8:
-                    g_quantize(i - 1)
-                for m in ws:
-                    w_interleave_vector(m)
+                if i > 1:
+                    g_quantize(i - 2)
                 weigh_turned(i - 1, 1)
-                for m in gs:
-                    g_interleave_vector(m)
-                if i == n - 1:
-                    h_quantize(i - 1, 0, P)
-                    h_quantize(i - 1, P, PAIR)
-                elif gs:
-                    h_quantize(i - 1, 0, PAIR)
-                    w_quantize(i + 2)
+                g_interleave_vector(i - 1)
+                h_quantize(i - 1, 0, PAIR)
+            elif i + 2 < n:
+                if turned(i - 2):
+                    g_quantize(i - 2)
                 else:
-                    w_quantize(i + 2)
-                    h_quantize(i - 1, 0, PAIR)
-            elif ws:
+                    h_quantize(i - 2, 0, PAIR)
                 add_direct(i - 1, 0, PAIR)
                 w_interleave_vector(i + 2)
                 weigh_direct(i - 1, 0, PAIR)
-                w_quantize(i + 2)
-                h_quantize(i - 1, 0, PAIR)
             else:
-                for a in range(2):
-                    add_direct(i - 1, a * P, (a + 1) * P)
-                for a in range(2):
-                    weigh_direct(i - 1, a * P, (a + 1) * P)
-                for a in range(2):
-                    h_quantize(i - 1, a * P, (a + 1) * P)
-            if i + 1 < n:
-                project(i + 1, 0)
-                project(i + 1, 1)
+                add_direct(i - 1, 0, PAIR)
+                h_quantize(i - 2, 0, PAIR)
+                weigh_direct(i - 1, 0, PAIR)
+            project(i + 1, 0)
+            project(i + 1, 1)
             if turned(i):
                 turn(i, 0)
                 turn(i, 1)
-            if i == 8:
-                r_transpose(3, banks[3])
-                r_copy(3, banks[3])
+            emit_passes(passes.get(i, []))
 
         last = n - 1
-        for j in (2, 3):
-            for vh in range(2):
-                grad_pass(banks[bank_of[6, vh]], 6, vh, j)
-        for vh in range(2):
-            grad_out(nc.scalar.copy, banks[bank_of[6, vh]], 6, vh)
-        weigh_turned(last, 0)
-        weigh_turned(last, 1)
-        for a in range(2):
-            h_quantize(last, a * P, (a + 1) * P)
-        for j in (2, 3):
-            for vh in range(2):
-                grad_pass(banks[bank_of[7, vh]], 7, vh, j)
-        grad_out(nc.scalar.copy, banks[bank_of[7, 0]], 7, 0)
-        grad_out(nc.vector.tensor_copy, banks[bank_of[7, 1]], 7, 1)
+        activate(last, 0)
+        activate(last, 1)
+        emit_out([(5, 0), (5, 1), (4, 0), (4, 1)])
+        add_direct(last - 1, 0, P)
+        h_quantize(last - 2, 0, PAIR)
+        add_direct(last - 1, P, PAIR)
+        weigh_direct(last - 1, 0, P)
+        weigh_direct(last - 1, P, PAIR)
+        add_direct(last, 0, P)
+        h_quantize(last - 1, 0, PAIR)
+        emit_passes([(6, vh, 1) for vh in (0, 1)] + [(7, vh, j) for j in (0, 1) for vh in (0, 1)])
+        emit_passes([(6, vh, j) for j in (2, 3) for vh in (0, 1)])
+        emit_out([(6, 0), (6, 1)])
+        add_direct(last, P, PAIR)
+        weigh_direct(last, 0, P)
+        weigh_direct(last, P, PAIR)
+        h_quantize(last, 0, P)
+        h_quantize(last, P, PAIR)
+        emit_passes([(7, vh, j) for j in (2, 3) for vh in (0, 1)])
+        grad_out(nc.vector.tensor_copy, banks[bank_of[7, 0]], 7, 0)
+        grad_out(nc.scalar.copy, banks[bank_of[7, 1]], 7, 1)

@@ -23,13 +23,13 @@ GROUPS = ([[(j, 2 * dp), (j, 2 * dp + 1)] for j in range(HEADS) for dp in (0, 1)
           + [[(j, 4), (j, 5)] for j in range(HEADS)] + [[(j, 6), (j, 7)] for j in (0, 1)]
           + [[(2, dt), (3, dt)] for dt in (6, 7)])
 TURNED = (0, 1, 2, 3, 4, 5, 6, 7)
-LOADS = "x0 x1 w000 w001 r0 c w100 w101 g0 w200 w201 g1 w300 w301 g2 g3 r1 w010 w011 w110 w111"
-W_SHARE = [512, 256, 512] + [256] * 7 + [208] * 4 + [128] * 2
-G_SHARE = [208] * 8
+LOADS = "x0 x1 x2 x3 w000 w001 g0 r0 c w100 w101 g1 w200 w201 g2 w300 w301 g3 r1 w010 w011 w110 w111"
+W_SHARE = [512, 256, 512] + [256] * 6 + [144] * 2 + [208] * 3 + [128] * 2
+G_SHARE = [256, 512] + [128] * 6
 W_RAW_TILES = 6
 SPLIT = 14
-RC_FIRST = False
-RC_S = True
+HELPED = (9, 10)
+G_HELP = 112
 OUT_TILES = 8
 
 
@@ -46,7 +46,7 @@ def tile_medusa_unembedding_grad_s7_kernel(tc, x, r, w, c, g, out):
         ident32 = sb.tile([P, P], F32, name="ident32", align_bytes=64)
         ident16 = sb.tile([P, P], BF16, name="ident16", align_bytes=64)
         warm = sb.tile([P, 2], F32, name="warm", align_bytes=64)
-        x_raw = tiles("x_raw", 2, [P, 2, D], BF16)
+        x_raw = tiles("x_raw", PACK, [P, D], BF16)
         r_raw = tiles("r_raw", 2, [P, PACK, BANK], BF16)
         c_tok = sb.tile([P, HEADS, 16], BF16, name="c_tok", align_bytes=64)
         w_raw = [tiles("w_raw%d_" % i, 2, [P, PACK, BANK], BF16) for i in range(W_RAW_TILES)]
@@ -89,7 +89,7 @@ def tile_medusa_unembedding_grad_s7_kernel(tc, x, r, w, c, g, out):
             nc.sync.dma_start(out=g_raw[j][:], in_=g[j * T:(j + 1) * T, :].rearrange("(p t) n -> p t n", t=PACK))
 
         def load_x(a):
-            nc.sync.dma_start(out=x_raw[a][:], in_=x.rearrange("(p t) n -> p t n", t=PACK)[:, 2 * a:2 * a + 2, :])
+            nc.sync.dma_start(out=x_raw[a][:], in_=x.rearrange("(p t) n -> p t n", t=PACK)[:, a, :])
 
         def load_r(half):
             nc.sync.dma_start(out=r_raw[half][:], in_=r[:, half * BANK:(half + 1) * BANK].rearrange("(p t) n -> p t n", t=PACK))
@@ -111,8 +111,15 @@ def tile_medusa_unembedding_grad_s7_kernel(tc, x, r, w, c, g, out):
             if W_SHARE[i] > PAIR:
                 w_interleave(nc.vector.tensor_copy, i, 1, 0, W_SHARE[i] - PAIR)
 
+        def w_interleave_gpsimd(i):
+            j, dt = GROUPS[i][0]
+            lo = W_SHARE[i] - 4
+            nc.gpsimd.tensor_scalar(out=w_grp[i % 3][:, 0, lo:PAIR, :],
+                                    in0=raw_w(j, dt // 4)[0][:, :, dt % 4 * P + lo:dt % 4 * P + PAIR].rearrange("p t n -> p n t"),
+                                    scalar1=1.0, scalar2=0.0, op0=MULT, op1=ADD)
+
         def w_interleave_scalar(i):
-            if W_SHARE[i] < PAIR:
+            if W_SHARE[i] < PAIR and i not in HELPED:
                 w_interleave(nc.scalar.copy, i, 0, W_SHARE[i], PAIR)
             if W_SHARE[i] < 2 * PAIR:
                 w_interleave(nc.scalar.copy, i, 1, max(W_SHARE[i] - PAIR, 0), PAIR)
@@ -125,17 +132,25 @@ def tile_medusa_unembedding_grad_s7_kernel(tc, x, r, w, c, g, out):
             j, vh = divmod(i, 2)
             interleave(nc.vector.tensor_copy, g_grp[i % 2][:, 0:G_SHARE[i], :], g_raw[j][:, :, vh * BANK:vh * BANK + G_SHARE[i]])
 
+        def g_interleave_gpsimd(i):
+            j, vh = divmod(i, 2)
+            lo, hi = G_SHARE[i] - 4, G_SHARE[i] + G_HELP
+            if G_HELP:
+                nc.gpsimd.tensor_scalar(out=g_grp[i % 2][:, lo:hi, :], in0=g_raw[j][:, :, vh * BANK + lo:vh * BANK + hi].rearrange("p t n -> p n t"),
+                                        scalar1=1.0, scalar2=0.0, op0=MULT, op1=ADD)
+
         def g_interleave_scalar(i):
             j, vh = divmod(i, 2)
-            if G_SHARE[i] < BANK:
-                interleave(nc.scalar.copy, g_grp[i % 2][:, G_SHARE[i]:BANK, :], g_raw[j][:, :, vh * BANK + G_SHARE[i]:(vh + 1) * BANK])
+            lo = G_SHARE[i] + (G_HELP if i >= 2 else 0)
+            if lo < BANK:
+                interleave(nc.scalar.copy, g_grp[i % 2][:, lo:BANK, :], g_raw[j][:, :, vh * BANK + lo:(vh + 1) * BANK])
 
         def g_quantize(i):
             j, vh = divmod(i, 2)
             quantize(g_codes[2 * j + vh][:], g_scales[2 * j + vh][:], g_grp[i % 2][:].rearrange("p n t -> p (n t)"))
 
         def x_transpose(t):
-            words = x_raw[t // 2][:, t % 2, :].bitcast(F32)
+            words = x_raw[t][:].bitcast(F32)
             for k in range(2):
                 for u in range(2):
                     q = 2 * k + u
@@ -237,14 +252,16 @@ def tile_medusa_unembedding_grad_s7_kernel(tc, x, r, w, c, g, out):
 
         bank_of = {(0, 0): 4, (0, 1): 5, (1, 0): 6, (1, 1): 7, (2, 0): 2, (3, 0): 3, (2, 1): 4, (3, 1): 6,
                    (4, 0): 5, (4, 1): 7, (5, 0): 2, (5, 1): 3, (6, 0): 4, (6, 1): 6, (7, 0): 2, (7, 1): 3}
-        passes = {i: [(dt, (i - 3) % 2, (i - 3) // 2) for dt in (0, 1)] for i in range(3, 11)}
+        passes = {i: [(dt, i % 2, i // 2 - 1) for dt in (0, 1)] for i in range(2, 10)}
+        passes[8] = passes[7] + passes[8]
+        passes[7] = []
         passes[9] = passes[9] + [(dt, 0, j) for dt in (2, 3) for j in range(HEADS)]
-        passes[10] = passes[10] + [(2, 1, j) for j in range(HEADS)]
-        passes[11] = [(3, 1, j) for j in range(HEADS)] + [(4, vh, j) for j in (0, 1) for vh in (0, 1)]
-        passes[12] = [(5, vh, j) for j in (0, 1) for vh in (0, 1)] + [(dt, vh, 2) for dt in (4, 5) for vh in (0, 1)]
+        passes[10] = [(dt, 1, j) for dt in (2, 3) for j in range(HEADS)]
+        passes[11] = [(4, vh, j) for j in (0, 1) for vh in (0, 1)] + [(5, vh, 0) for vh in (0, 1)]
+        passes[12] = [(5, vh, 1) for vh in (0, 1)] + [(dt, vh, 2) for dt in (4, 5) for vh in (0, 1)]
         passes[13] = [(dt, vh, 3) for dt in (5, 4) for vh in (0, 1)]
         passes[14] = [(6, vh, 0) for vh in (0, 1)]
-        outs = {10: [(0, 0), (1, 0)], 11: [(0, 1), (1, 1)], 12: [(2, 0), (3, 0)], 13: [(2, 1)], 14: [(3, 1)]}
+        outs = {9: [(0, 0), (1, 0)], 10: [(0, 1), (1, 1)], 11: [(2, 0), (3, 0)], 12: [(2, 1)], 13: [(3, 1)]}
 
         ctx.enter_context(tc.manual_schedule())
 
@@ -267,33 +284,37 @@ def tile_medusa_unembedding_grad_s7_kernel(tc, x, r, w, c, g, out):
 
         for t in range(PACK):
             x_transpose(t)
-        for t in range(PACK):
-            x_copy(nc.scalar.copy, t)
-        r_transpose(0, banks[2])
-        r_transpose(1, banks[3])
-        w_interleave_vector(0)
-        w_interleave_vector(1)
-        if RC_FIRST:
-            r_copy(nc.scalar.copy, 0, banks[2])
-        w_interleave_scalar(0)
-        w_interleave_scalar(1)
+        x_copy(nc.scalar.copy, 0)
+        x_copy(nc.scalar.copy, 1)
+        x_copy(nc.scalar.copy, 2)
+        x_copy(nc.scalar.copy, 3)
+        w_interleave(nc.vector.tensor_copy, 0, 0, 0, PAIR)
+        w_interleave(nc.vector.tensor_copy, 1, 0, 0, PAIR)
+        w_interleave(nc.vector.tensor_copy, 0, 1, 0, PAIR)
+        w_interleave(nc.scalar.copy, 1, 1, 0, PAIR)
         x_quantize(0)
         w_quantize(0)
         x_quantize(1)
         project(0, 0)
         project(0, 1)
-        if not RC_FIRST:
-            r_copy(nc.scalar.copy, 0, banks[2])
+        g_interleave_scalar(0)
         w_quantize(1)
-        r_copy(nc.scalar.copy if RC_S else nc.vector.tensor_copy, 1, banks[3])
+        g_interleave_vector(0)
+        r_transpose(0, banks[4])
+        r_transpose(1, banks[5])
         activate(0, 0)
         activate(0, 1)
-        w_interleave_vector(2)
-        w_interleave_scalar(2)
+        r_copy(nc.scalar.copy, 0, banks[4])
+        g_interleave_vector(1)
+        g_quantize(0)
         project(1, 0)
         project(1, 1)
         turn(0, 0)
         turn(0, 1)
+        w_interleave_vector(2)
+        g_interleave_scalar(1)
+        w_interleave_scalar(2)
+        r_copy(nc.scalar.copy, 1, banks[5])
 
         n = len(GROUPS)
         for i in range(1, n - 1):
@@ -305,22 +326,26 @@ def tile_medusa_unembedding_grad_s7_kernel(tc, x, r, w, c, g, out):
             emit_out(outs.get(i, []))
             if i + 2 < n:
                 w_interleave_scalar(i + 2)
-            if i <= 8:
-                g_interleave_scalar(i - 1)
+            if i + 1 < 8:
+                g_interleave_scalar(i + 1)
             w_quantize(i + 1)
             if turned(i - 1):
-                w_interleave_vector(i + 2)
-                weigh_turned(i - 1, 0)
-                if i > 1:
-                    g_quantize(i - 2)
-                weigh_turned(i - 1, 1)
-                g_interleave_vector(i - 1)
-                h_quantize(i - 1, 0, PAIR)
-            elif i + 2 < n:
-                if turned(i - 2):
-                    g_quantize(i - 2)
-                else:
+                if i >= 2:
                     h_quantize(i - 2, 0, PAIR)
+                if i + 1 < 8:
+                    w_interleave_vector(i + 2)
+                    g_quantize(i)
+                    g_interleave_vector(i + 1)
+                    g_interleave_gpsimd(i + 1)
+                else:
+                    if i < 8:
+                        g_quantize(i)
+                    w_interleave_vector(i + 2)
+                    w_interleave_gpsimd(i + 2)
+                weigh_turned(i - 1, 0)
+                weigh_turned(i - 1, 1)
+            elif i + 2 < n:
+                h_quantize(i - 2, 0, PAIR)
                 add_direct(i - 1, 0, PAIR)
                 w_interleave_vector(i + 2)
                 weigh_direct(i - 1, 0, PAIR)
@@ -330,10 +355,10 @@ def tile_medusa_unembedding_grad_s7_kernel(tc, x, r, w, c, g, out):
                 weigh_direct(i - 1, 0, PAIR)
             project(i + 1, 0)
             project(i + 1, 1)
+            emit_passes(passes.get(i, []))
             if turned(i):
                 turn(i, 0)
                 turn(i, 1)
-            emit_passes(passes.get(i, []))
 
         last = n - 1
         activate(last, 0)

@@ -17,20 +17,40 @@ SILU = mybir.ActivationFunctionType.Silu
 
 P = 128
 PACK = 4
+K_PASS = P * PACK
 BANK = 512
-PAIR = 256
-GROUPS = ([[(j, 2 * dp), (j, 2 * dp + 1)] for j in range(HEADS) for dp in (0, 1)]
+WIDTH = 2 * P
+
+GROUPS = ([[(j, 2 * pair), (j, 2 * pair + 1)] for j in range(HEADS) for pair in (0, 1)]
           + [[(j, 4), (j, 5)] for j in range(HEADS)] + [[(j, 6), (j, 7)] for j in (0, 1)]
-          + [[(2, dt), (3, dt)] for dt in (6, 7)])
-TURNED = (0, 1, 2, 3, 4, 5, 6, 7)
-LOADS = "x0 x1 x2 x3 w000 w001 g0 r0 c w100 w101 g1 w200 w201 g2 w300 w301 g3 r1 w010 w011 w110 w111"
-W_SHARE = [512, 256, 512] + [256] * 6 + [144] * 2 + [208] * 3 + [128] * 2
-G_SHARE = [256, 512] + [128] * 6
-W_RAW_TILES = 6
-SPLIT = 14
-HELPED = (9, 10)
-G_HELP = 112
-OUT_TILES = 8
+          + [[(2, tile), (3, tile)] for tile in (6, 7)])
+TURNED = 8
+TWO_HEADS = 14
+G_PIECES = 2 * HEADS
+
+G_VECTOR, G_GPSIMD = 176, 112
+G_FIRST_VECTOR = 256
+W_HELPED = 9
+W_VECTOR = 144
+OVERLAP = 4
+
+W_RAW, W_RING, G_RING, H_RING = 6, 3, 2, 2
+SILU_TURNED_RING, SILU_DIRECT_RING, DU_RING = 4, 3, 8
+
+Z_BANKS, SUM_BANKS, C_BANK = (0, 1), (2, 3), 2
+X_BANKS, R_BANKS, C_ROWS_BANK = (4, 5, 6, 7), (4, 5), 7
+DU_BANK = {(0, 0): 4, (0, 1): 5, (1, 0): 6, (1, 1): 7, (2, 0): 3, (3, 0): 4, (2, 1): 6, (3, 1): 5,
+           (4, 0): 7, (4, 1): 3, (5, 0): 4, (5, 1): 6, (6, 0): 5, (6, 1): 4, (7, 0): 6, (7, 1): 7}
+PASSES = dict([(step, [(tile, step % 2, step // 2 - 1) for tile in (0, 1)]) for step in range(2, 7)] + [
+    (8, [(tile, 1, 2) for tile in (0, 1)] + [(tile, 0, 3) for tile in (0, 1)]),
+    (9, [(tile, 1, 3) for tile in (0, 1)] + [(tile, 0, j) for tile in (2, 3) for j in range(HEADS)]),
+    (10, [(tile, 1, j) for tile in (2, 3) for j in range(HEADS)]),
+    (11, [(tile, half, j) for j in (0, 1) for tile, half in ((4, 0), (4, 1), (5, 0))]),
+    (12, [(5, 1, j) for j in (0, 1)] + [(tile, half, 2) for tile in (4, 5) for half in (0, 1)]),
+    (13, [(tile, half, 3) for tile in (5, 4) for half in (0, 1)]),
+    (14, [(6, half, 0) for half in (0, 1)]),
+])
+OUTS = {9: [(0, 0), (1, 0)], 10: [(0, 1), (1, 1)], 11: [(2, 0), (3, 0)], 12: [(2, 1)], 13: [(3, 1)], 14: [(5, 0)]}
 
 
 def tile_medusa_unembedding_grad_s7_kernel(tc, x, r, w, c, g, out):
@@ -48,172 +68,154 @@ def tile_medusa_unembedding_grad_s7_kernel(tc, x, r, w, c, g, out):
         warm = sb.tile([P, 2], F32, name="warm", align_bytes=64)
         x_raw = tiles("x_raw", PACK, [P, D], BF16)
         r_raw = tiles("r_raw", 2, [P, PACK, BANK], BF16)
-        c_tok = sb.tile([P, HEADS, 16], BF16, name="c_tok", align_bytes=64)
-        w_raw = [tiles("w_raw%d_" % i, 2, [P, PACK, BANK], BF16) for i in range(W_RAW_TILES)]
+        c_tok = sb.tile([P, 8, 16], BF16, name="c_tok", align_bytes=64)
+        c_rows = sb.tile([P, P], BF16, name="c_rows", align_bytes=64)
+        w_raw = [tiles("w_raw%d_" % i, 2, [P, PACK, BANK], BF16) for i in range(W_RAW)]
         g_raw = tiles("g_raw", HEADS, [P, PACK, V], BF16)
-        x_grp = sb.tile([P, 2, T, PACK], BF16, name="x_grp", align_bytes=64)
-        w_grp = tiles("w_grp", 3, [P, 2, PAIR, PACK], BF16)
-        g_grp = tiles("g_grp", 2, [P, BANK, PACK], BF16)
+        x_grouped = sb.tile([P, 2, T, PACK], BF16, name="x_grouped", align_bytes=64)
+        w_grouped = tiles("w_grouped", W_RING, [P, 2, WIDTH, PACK], BF16)
+        g_grouped = tiles("g_grouped", G_RING, [P, BANK, PACK], BF16)
         x_codes = tiles("x_codes", 2, [P, T], U32)
         x_scales = tiles("x_scales", 2, [P, T], U8)
-        w_codes = tiles("w_codes", 3, [P, 2, PAIR], U32)
-        w_scales = tiles("w_scales", 3, [P, 2, PAIR], U8)
-        g_codes = tiles("g_codes", 8, [P, BANK], U32)
-        g_scales = tiles("g_scales", 8, [P, BANK], U8)
-        h_codes = tiles("h_codes", 16, [P, PAIR], U32)
-        h_scales = tiles("h_scales", 16, [P, PAIR], U8)
-        silu = tiles("silu", 4, [P, BANK], F32)
-        silu2 = tiles("silu2_", 3, [P, 2 * BANK], F32)
-        h_grp = tiles("h_grp", 2, [P, PAIR, PACK], BF16)
+        w_codes = tiles("w_codes", W_RING, [P, 2, WIDTH], U32)
+        w_scales = tiles("w_scales", W_RING, [P, 2, WIDTH], U8)
+        g_codes = tiles("g_codes", G_PIECES, [P, BANK], U32)
+        g_scales = tiles("g_scales", G_PIECES, [P, BANK], U8)
+        h_codes = tiles("h_codes", len(GROUPS), [P, WIDTH], U32)
+        h_scales = tiles("h_scales", len(GROUPS), [P, WIDTH], U8)
+        silu_turned = tiles("silu_turned", SILU_TURNED_RING, [P, T], F32)
+        silu_direct = tiles("silu_direct", SILU_DIRECT_RING, [P, WIDTH * PACK], F32)
+        h_grouped = tiles("h_grouped", H_RING, [P, WIDTH, PACK], BF16)
         r_turned = tiles("r_turned", 2, [P, 2, T], F32)
-        du = tiles("du", OUT_TILES, [P, BANK], F32)
+        du = tiles("du", DU_RING, [P, BANK], F32)
 
-        def interleave(copy, dst, src):
-            copy(out=dst.rearrange("p (c i) t -> p c t i", i=4), in_=src.rearrange("p t (c i) -> p c t i", i=4))
+        def raw_w(j, half):
+            return w_raw[(half * HEADS + j) % W_RAW]
+
+        def four_rows(rows):
+            return rows.rearrange("(p t) n -> p t n", t=PACK)
+
+        def load_w(j, half):
+            cols = slice(j * D + half * BANK, j * D + (half + 1) * BANK)
+            for k in range(2):
+                nc.sync.dma_start(out=raw_w(j, half)[k][:], in_=four_rows(w[k * K_PASS:(k + 1) * K_PASS, cols]))
+
+        def load_g(j):
+            nc.sync.dma_start(out=g_raw[j][:], in_=four_rows(g[j * T:(j + 1) * T, :]))
+
+        def load_r(half):
+            nc.sync.dma_start(out=r_raw[half][:], in_=four_rows(r[:, half * BANK:(half + 1) * BANK]))
+
+        def interleave(copy, grouped, raw):
+            copy(out=grouped.rearrange("p (n i) t -> p n t i", i=4), in_=raw.rearrange("p t (n i) -> p n t i", i=4))
+
+        def interleave_gpsimd(grouped, raw):
+            nc.gpsimd.tensor_scalar(out=grouped, in0=raw.rearrange("p t n -> p n t"), scalar1=1.0, scalar2=0.0, op0=MULT, op1=ADD)
 
         def quantize(codes, scales, grouped):
             nc.vector.quantize_mx(out=codes.bitcast(FP8X4), scales=scales, in_=grouped)
 
-        def mx(acc, lhs_codes, lhs_scales, rhs_codes, rhs_scales, start, stop):
-            nc.tensor.matmul_mx(out=acc, lhsT=lhs_codes.bitcast(FP8X4), lhsT_scale=lhs_scales,
-                                rhs=rhs_codes.bitcast(FP8X4), rhs_scale=rhs_scales, start=start, stop=stop)
+        def w_part(i, k, lo, hi):
+            j, tile = GROUPS[i][lo // P]
+            base = tile % 4 * P - lo // P * P
+            return w_grouped[i % W_RING][:, k, lo:hi, :], raw_w(j, tile // 4)[k][:, :, base + lo:base + hi]
 
-        def raw_w(j, half):
-            return w_raw[(half * HEADS + j) % W_RAW_TILES]
-
-        def load_w(j, half, k):
-            cols = slice(j * D + half * BANK, j * D + (half + 1) * BANK)
-            nc.sync.dma_start(out=raw_w(j, half)[k][:], in_=w[k * 512:(k + 1) * 512, cols].rearrange("(p t) n -> p t n", t=PACK))
-
-        def load_g(j):
-            nc.sync.dma_start(out=g_raw[j][:], in_=g[j * T:(j + 1) * T, :].rearrange("(p t) n -> p t n", t=PACK))
-
-        def load_x(a):
-            nc.sync.dma_start(out=x_raw[a][:], in_=x.rearrange("(p t) n -> p t n", t=PACK)[:, a, :])
-
-        def load_r(half):
-            nc.sync.dma_start(out=r_raw[half][:], in_=r[:, half * BANK:(half + 1) * BANK].rearrange("(p t) n -> p t n", t=PACK))
-
-        def turned(i):
-            return i in TURNED
-
-        def w_interleave(copy, i, k, lo, hi):
-            (j0, dt0), (j1, dt1) = GROUPS[i]
-            cuts = [lo, hi] if j0 == j1 or hi <= P or lo >= P else [lo, P, hi]
-            for a, b in zip(cuts, cuts[1:]):
-                j, dt = GROUPS[i][a // P]
-                base = dt % 4 * P - a // P * P
-                interleave(copy, w_grp[i % 3][:, k, a:b, :], raw_w(j, dt // 4)[k][:, :, base + a:base + b])
-
-        def w_interleave_vector(i):
-            if W_SHARE[i]:
-                w_interleave(nc.vector.tensor_copy, i, 0, 0, min(W_SHARE[i], PAIR))
-            if W_SHARE[i] > PAIR:
-                w_interleave(nc.vector.tensor_copy, i, 1, 0, W_SHARE[i] - PAIR)
-
-        def w_interleave_gpsimd(i):
-            j, dt = GROUPS[i][0]
-            lo = W_SHARE[i] - 4
-            nc.gpsimd.tensor_scalar(out=w_grp[i % 3][:, 0, lo:PAIR, :],
-                                    in0=raw_w(j, dt // 4)[0][:, :, dt % 4 * P + lo:dt % 4 * P + PAIR].rearrange("p t n -> p n t"),
-                                    scalar1=1.0, scalar2=0.0, op0=MULT, op1=ADD)
-
-        def w_interleave_scalar(i):
-            if W_SHARE[i] < PAIR and i not in HELPED:
-                w_interleave(nc.scalar.copy, i, 0, W_SHARE[i], PAIR)
-            if W_SHARE[i] < 2 * PAIR:
-                w_interleave(nc.scalar.copy, i, 1, max(W_SHARE[i] - PAIR, 0), PAIR)
+        def w_interleave(copy, i, k, cols):
+            cuts = [0, P, cols] if i >= TWO_HEADS else [0, cols]
+            for lo, hi in zip(cuts, cuts[1:]):
+                interleave(copy, *w_part(i, k, lo, hi))
 
         def w_quantize(i):
-            quantize(w_codes[i % 3][:].rearrange("p k n -> p (k n)"), w_scales[i % 3][:].rearrange("p k n -> p (k n)"),
-                     w_grp[i % 3][:].rearrange("p k n t -> p (k n t)"))
+            quantize(w_codes[i % W_RING][:].rearrange("p k n -> p (k n)"), w_scales[i % W_RING][:].rearrange("p k n -> p (k n)"),
+                     w_grouped[i % W_RING][:].rearrange("p k n t -> p (k n t)"))
 
-        def g_interleave_vector(i):
-            j, vh = divmod(i, 2)
-            interleave(nc.vector.tensor_copy, g_grp[i % 2][:, 0:G_SHARE[i], :], g_raw[j][:, :, vh * BANK:vh * BANK + G_SHARE[i]])
+        def g_part(m, lo, hi):
+            j, half = divmod(m, 2)
+            return g_grouped[m % G_RING][:, lo:hi, :], g_raw[j][:, :, half * BANK + lo:half * BANK + hi]
 
-        def g_interleave_gpsimd(i):
-            j, vh = divmod(i, 2)
-            lo, hi = G_SHARE[i] - 4, G_SHARE[i] + G_HELP
-            if G_HELP:
-                nc.gpsimd.tensor_scalar(out=g_grp[i % 2][:, lo:hi, :], in0=g_raw[j][:, :, vh * BANK + lo:vh * BANK + hi].rearrange("p t n -> p n t"),
-                                        scalar1=1.0, scalar2=0.0, op0=MULT, op1=ADD)
-
-        def g_interleave_scalar(i):
-            j, vh = divmod(i, 2)
-            lo = G_SHARE[i] + (G_HELP if i >= 2 else 0)
-            if lo < BANK:
-                interleave(nc.scalar.copy, g_grp[i % 2][:, lo:BANK, :], g_raw[j][:, :, vh * BANK + lo:(vh + 1) * BANK])
-
-        def g_quantize(i):
-            j, vh = divmod(i, 2)
-            quantize(g_codes[2 * j + vh][:], g_scales[2 * j + vh][:], g_grp[i % 2][:].rearrange("p n t -> p (n t)"))
+        def g_quantize(m):
+            quantize(g_codes[m][:], g_scales[m][:], g_grouped[m % G_RING][:].rearrange("p n t -> p (n t)"))
 
         def x_transpose(t):
             words = x_raw[t][:].bitcast(F32)
             for k in range(2):
                 for u in range(2):
                     q = 2 * k + u
-                    nc.tensor.transpose(banks[4 + t][:, q * P:(q + 1) * P], words[:, 256 * k + u:256 * (k + 1):2], ident32[:])
+                    nc.tensor.transpose(banks[X_BANKS[t]][:, q * P:(q + 1) * P], words[:, 2 * P * k + u:2 * P * (k + 1):2], ident32[:])
 
-        def x_copy(copy, t):
-            dst = x_grp[:, :, t * P:(t + 1) * P, :].rearrange("p k m t -> p k (m t)").bitcast(F32).rearrange("p k (m u) -> p k m u", u=2)
-            copy(out=dst, in_=banks[4 + t][:].rearrange("p (k u m) -> p k m u", k=2, u=2))
+        def x_copy(t):
+            grouped = x_grouped[:, :, t * P:(t + 1) * P, :].rearrange("p k m t -> p k (m t)").bitcast(F32)
+            nc.scalar.copy(out=grouped.rearrange("p k (m u) -> p k m u", u=2),
+                           in_=banks[X_BANKS[t]][:].rearrange("p (k u m) -> p k m u", k=2, u=2))
 
         def x_quantize(k):
-            quantize(x_codes[k][:], x_scales[k][:], x_grp[:, k, :, :].rearrange("p n t -> p (n t)"))
+            quantize(x_codes[k][:], x_scales[k][:], x_grouped[:, k, :, :].rearrange("p n t -> p (n t)"))
 
-        def r_transpose(dp, bank):
-            view = bank[:].bitcast(BF16)
+        def r_transpose(pair):
+            view = banks[R_BANKS[pair]][:].bitcast(BF16)
             for a in range(2):
                 for t in range(PACK):
                     q = a * PACK + t
-                    col = (dp % 2) * PAIR + a * P
-                    nc.tensor.transpose(view[:, q * P:(q + 1) * P], r_raw[dp // 2][:, t, col:col + P], ident16[:])
+                    col = pair * WIDTH + a * P
+                    nc.tensor.transpose(view[:, q * P:(q + 1) * P], r_raw[0][:, t, col:col + P], ident16[:])
 
-        def r_copy(copy, dp, bank):
-            copy(out=r_turned[dp % 2][:].rearrange("p a n -> p (a n)"), in_=bank[:].bitcast(BF16))
+        def r_copy(pair):
+            nc.scalar.copy(out=r_turned[pair][:].rearrange("p a n -> p (a n)"), in_=banks[R_BANKS[pair]][:].bitcast(BF16))
 
-        def project(i, a):
-            for t in ((None,) if turned(i) else (2 * a, 2 * a + 1)):
-                for k in range(2):
-                    if turned(i):
-                        cols = slice(a * P, (a + 1) * P)
-                        mx(banks[a][:], w_codes[i % 3][:, k, cols], w_scales[i % 3][:, k, cols],
-                           x_codes[k][:], x_scales[k][:], k == 0, k == 1)
-                    else:
-                        cols = slice(t * P, (t + 1) * P)
-                        mx(banks[a][:, t % 2 * PAIR:(t % 2 + 1) * PAIR], x_codes[k][:, cols], x_scales[k][:, cols],
-                           w_codes[i % 3][:, k, :], w_scales[i % 3][:, k, :], k == 0, k == 1)
+        def square16(bank):
+            return banks[bank][:].bitcast(BF16)[:, 0:P]
 
-        def activate(i, a):
-            if turned(i):
-                nc.scalar.activation(out=silu[(2 * i + a) % 4][:], in_=banks[a][:], func=SILU)
-            else:
-                parts = 2 if i >= SPLIT else 1
-                nc.scalar.activation(out=silu2[i % 3][:].rearrange("p (b a n e) -> p b a n e", b=parts, a=2, e=2)[:, :, a, :, :],
-                                     in_=banks[a][:].rearrange("p (e b n) -> p b n e", e=2, b=parts), func=SILU)
+        def mx(acc, lhs_codes, lhs_scales, rhs_codes, rhs_scales, start, stop):
+            nc.tensor.matmul_mx(out=acc, lhsT=lhs_codes.bitcast(FP8X4), lhsT_scale=lhs_scales,
+                                rhs=rhs_codes.bitcast(FP8X4), rhs_scale=rhs_scales, start=start, stop=stop)
 
-        def turn_bank(i, a):
-            return banks[2 + a]
+        def project(i):
+            codes, scales = w_codes[i % W_RING], w_scales[i % W_RING]
+            for a in range(2):
+                bank = banks[Z_BANKS[a]]
+                if i < TURNED:
+                    cols = slice(a * P, (a + 1) * P)
+                    for k in range(2):
+                        mx(bank[:], codes[:, k, cols], scales[:, k, cols], x_codes[k][:], x_scales[k][:], k == 0, k == 1)
+                else:
+                    for e in range(2):
+                        cols = slice((2 * a + e) * P, (2 * a + e + 1) * P)
+                        for k in range(2):
+                            mx(bank[:, e * WIDTH:(e + 1) * WIDTH], x_codes[k][:, cols], x_scales[k][:, cols],
+                               codes[:, k, :], scales[:, k, :], k == 0, k == 1)
 
-        def turn(i, a):
-            dt = GROUPS[i][a][1]
-            for t in range(PACK):
-                cols = slice(t * P, (t + 1) * P)
-                acc = turn_bank(i, a)[:, cols]
-                nc.tensor.matmul(acc, lhsT=r_turned[dt // 2 % 2][:, dt % 2, cols], rhs=ident32[:], start=True, stop=False, is_transpose=True)
-                nc.tensor.matmul(acc, lhsT=silu[(2 * i + a) % 4][:, cols], rhs=ident32[:], start=False, stop=True, is_transpose=True)
+        def activate(i):
+            for a in range(2):
+                bank = banks[Z_BANKS[a]]
+                if i < TURNED:
+                    nc.scalar.activation(out=silu_turned[(2 * i + a) % SILU_TURNED_RING][:], in_=bank[:], func=SILU)
+                else:
+                    heads = 2 if i >= TWO_HEADS else 1
+                    parts = silu_direct[i % SILU_DIRECT_RING][:].rearrange("p (b a n e) -> p b a n e", b=heads, a=2, e=2)
+                    nc.scalar.activation(out=parts[:, :, a, :, :], in_=bank[:].rearrange("p (e b n) -> p b n e", e=2, b=heads), func=SILU)
 
-        def c_spread(i, a, n):
-            return c_tok[:, GROUPS[i][a][0], 0:PACK].unsqueeze(1).to_broadcast([P, n, PACK])
+        def turn(i):
+            for a in range(2):
+                tile = GROUPS[i][a][1]
+                for t in range(PACK):
+                    cols = slice(t * P, (t + 1) * P)
+                    acc = banks[SUM_BANKS[a]][:, cols]
+                    nc.tensor.matmul(acc, lhsT=r_turned[tile // 2][:, tile % 2, cols], rhs=ident32[:],
+                                     start=True, stop=False, is_transpose=True)
+                    nc.tensor.matmul(acc, lhsT=silu_turned[(2 * i + a) % SILU_TURNED_RING][:, cols], rhs=ident32[:],
+                                     start=False, stop=True, is_transpose=True)
 
-        def weigh_turned(i, a):
-            nc.vector.tensor_tensor(out=h_grp[i % 2][:, a * P:(a + 1) * P, :], in0=turn_bank(i, a)[:].rearrange("p (t n) -> p n t", t=PACK),
-                                    in1=c_spread(i, a, P), op=MULT)
+        def c_spread(table, j, n):
+            return table[:, j, 0:PACK].unsqueeze(1).to_broadcast([P, n, PACK])
+
+        def weigh_turned(i):
+            for a in range(2):
+                nc.vector.tensor_tensor(out=h_grouped[i % H_RING][:, a * P:(a + 1) * P, :],
+                                        in0=banks[SUM_BANKS[a]][:].rearrange("p (t n) -> p n t", t=PACK),
+                                        in1=c_spread(c_tok[:], GROUPS[i][a][0], P), op=MULT)
 
         def silu_part(i, lo, hi):
-            return silu2[i % 3][:, lo * PACK:hi * PACK].rearrange("p (a n e) -> p a n e", a=2, e=2)
+            return silu_direct[i % SILU_DIRECT_RING][:, lo * PACK:hi * PACK].rearrange("p (a n e) -> p a n e", a=2, e=2)
 
         def add_direct(i, lo, hi):
             base = GROUPS[i][lo // P][1] % 4 * P - lo // P * P
@@ -221,61 +223,46 @@ def tile_medusa_unembedding_grad_s7_kernel(tc, x, r, w, c, g, out):
                                     in1=r_raw[1][:, :, base + lo:base + hi].rearrange("p (a e) n -> p a n e", e=2), op=ADD)
 
         def weigh_direct(i, lo, hi):
-            nc.vector.tensor_tensor(out=h_grp[i % 2][:, lo:hi, :].rearrange("p n (a e) -> p n a e", e=2),
+            table = square16(C_BANK).rearrange("p (j t) -> p j t", t=16)
+            nc.vector.tensor_tensor(out=h_grouped[i % H_RING][:, lo:hi, :].rearrange("p n (a e) -> p n a e", e=2),
                                     in0=silu_part(i, lo, hi).rearrange("p a n e -> p n a e"),
-                                    in1=c_spread(i, lo // P, hi - lo).rearrange("p n (a e) -> p n a e", e=2), op=MULT)
+                                    in1=c_spread(table, GROUPS[i][lo // P][0], hi - lo).rearrange("p n (a e) -> p n a e", e=2), op=MULT)
 
         def h_quantize(i, lo, hi):
-            quantize(h_codes[i][:, lo:hi], h_scales[i][:, lo:hi], h_grp[i % 2][:, lo:hi, :].rearrange("p n t -> p (n t)"))
+            quantize(h_codes[i][:, lo:hi], h_scales[i][:, lo:hi], h_grouped[i % H_RING][:, lo:hi, :].rearrange("p n t -> p (n t)"))
 
-        def grad_pass(bank, dt, vh, j):
-            i, a = [(m, units.index((j, dt))) for m, units in enumerate(GROUPS) if (j, dt) in units][0]
-            cols = slice(a * P, (a + 1) * P)
-            mx(bank[:], h_codes[i][:, cols], h_scales[i][:, cols], g_codes[2 * j + vh][:], g_scales[2 * j + vh][:],
-               j == 0, j == HEADS - 1)
-
+        place = {unit: (i, a) for i, units in enumerate(GROUPS) for a, unit in enumerate(units)}
         stored = []
 
-        def grad_out(copy, bank, dt, vh):
-            stage = du[len(stored) % OUT_TILES]
-            stored.append((dt, vh))
-            copy(out=stage[:], in_=bank[:])
-            nc.sync.dma_start(out=out[dt * P:(dt + 1) * P, vh * BANK:(vh + 1) * BANK], in_=stage[:])
+        def grad_passes(todo):
+            for tile, half, j in todo:
+                i, a = place[j, tile]
+                cols = slice(a * P, (a + 1) * P)
+                mx(banks[DU_BANK[tile, half]][:], h_codes[i][:, cols], h_scales[i][:, cols],
+                   g_codes[2 * j + half][:], g_scales[2 * j + half][:], j == 0, j == HEADS - 1)
 
-        def emit_passes(todo):
-            for dt, vh, j in todo:
-                grad_pass(banks[bank_of[dt, vh]], dt, vh, j)
-
-        def emit_out(todo):
-            for dt, vh in todo:
-                grad_out(nc.scalar.copy, banks[bank_of[dt, vh]], dt, vh)
-
-        bank_of = {(0, 0): 4, (0, 1): 5, (1, 0): 6, (1, 1): 7, (2, 0): 2, (3, 0): 3, (2, 1): 4, (3, 1): 6,
-                   (4, 0): 5, (4, 1): 7, (5, 0): 2, (5, 1): 3, (6, 0): 4, (6, 1): 6, (7, 0): 2, (7, 1): 3}
-        passes = {i: [(dt, i % 2, i // 2 - 1) for dt in (0, 1)] for i in range(2, 10)}
-        passes[8] = passes[7] + passes[8]
-        passes[7] = []
-        passes[9] = passes[9] + [(dt, 0, j) for dt in (2, 3) for j in range(HEADS)]
-        passes[10] = [(dt, 1, j) for dt in (2, 3) for j in range(HEADS)]
-        passes[11] = [(4, vh, j) for j in (0, 1) for vh in (0, 1)] + [(5, vh, 0) for vh in (0, 1)]
-        passes[12] = [(5, vh, 1) for vh in (0, 1)] + [(dt, vh, 2) for dt in (4, 5) for vh in (0, 1)]
-        passes[13] = [(dt, vh, 3) for dt in (5, 4) for vh in (0, 1)]
-        passes[14] = [(6, vh, 0) for vh in (0, 1)]
-        outs = {9: [(0, 0), (1, 0)], 10: [(0, 1), (1, 1)], 11: [(2, 0), (3, 0)], 12: [(2, 1)], 13: [(3, 1)]}
+        def grad_out(copy, todo):
+            for tile, half in todo:
+                stage = du[len(stored) % DU_RING]
+                stored.append((tile, half))
+                copy(out=stage[:], in_=banks[DU_BANK[tile, half]][:])
+                nc.sync.dma_start(out=out[tile * P:(tile + 1) * P, half * BANK:(half + 1) * BANK], in_=stage[:])
 
         ctx.enter_context(tc.manual_schedule())
 
-        for name in LOADS.split():
-            if name[0] == "x":
-                load_x(int(name[1]))
-            if name[0] == "r":
-                load_r(int(name[1]))
-            if name[0] == "g":
-                load_g(int(name[1]))
-            if name[0] == "w":
-                load_w(int(name[1]), int(name[2]), int(name[3]))
-            if name[0] == "c":
-                nc.sync.dma_start(out=c_tok[:, :, 0:PACK], in_=c.rearrange("j (p t) -> p j t", t=PACK))
+        nc.vector.memset(c_tok[:], 0.0)
+        for t in range(PACK):
+            nc.sync.dma_start(out=x_raw[t][:], in_=four_rows(x)[:, t, :])
+        load_w(0, 0)
+        load_g(0)
+        load_r(0)
+        nc.sync.dma_start(out=c_tok[:, 0:HEADS, 0:PACK], in_=c.rearrange("j (p t) -> p j t", t=PACK))
+        for j in range(1, HEADS):
+            load_w(j, 0)
+            load_g(j)
+        load_r(1)
+        for j in range(W_RAW - HEADS):
+            load_w(j, 1)
 
         make_identity(nc, ident32[:])
         make_identity(nc, ident16[:])
@@ -284,101 +271,100 @@ def tile_medusa_unembedding_grad_s7_kernel(tc, x, r, w, c, g, out):
 
         for t in range(PACK):
             x_transpose(t)
-        x_copy(nc.scalar.copy, 0)
-        x_copy(nc.scalar.copy, 1)
-        x_copy(nc.scalar.copy, 2)
-        x_copy(nc.scalar.copy, 3)
-        w_interleave(nc.vector.tensor_copy, 0, 0, 0, PAIR)
-        w_interleave(nc.vector.tensor_copy, 1, 0, 0, PAIR)
-        w_interleave(nc.vector.tensor_copy, 0, 1, 0, PAIR)
-        w_interleave(nc.scalar.copy, 1, 1, 0, PAIR)
+        for t in range(PACK):
+            x_copy(t)
+        w_interleave(nc.vector.tensor_copy, 0, 0, WIDTH)
+        w_interleave(nc.vector.tensor_copy, 1, 0, WIDTH)
+        w_interleave(nc.vector.tensor_copy, 0, 1, WIDTH)
+        w_interleave(nc.scalar.copy, 1, 1, WIDTH)
         x_quantize(0)
         w_quantize(0)
         x_quantize(1)
-        project(0, 0)
-        project(0, 1)
-        g_interleave_scalar(0)
+        project(0)
+        interleave(nc.scalar.copy, *g_part(0, G_FIRST_VECTOR, BANK))
         w_quantize(1)
-        g_interleave_vector(0)
-        r_transpose(0, banks[4])
-        r_transpose(1, banks[5])
-        activate(0, 0)
-        activate(0, 1)
-        r_copy(nc.scalar.copy, 0, banks[4])
-        g_interleave_vector(1)
+        interleave(nc.vector.tensor_copy, *g_part(0, 0, G_FIRST_VECTOR))
+        r_transpose(0)
+        r_transpose(1)
+        activate(0)
+        r_copy(0)
+        interleave(nc.vector.tensor_copy, *g_part(1, 0, BANK))
         g_quantize(0)
-        project(1, 0)
-        project(1, 1)
-        turn(0, 0)
-        turn(0, 1)
-        w_interleave_vector(2)
-        g_interleave_scalar(1)
-        w_interleave_scalar(2)
-        r_copy(nc.scalar.copy, 1, banks[5])
+        project(1)
+        turn(0)
+        w_interleave(nc.vector.tensor_copy, 2, 0, WIDTH)
+        w_interleave(nc.vector.tensor_copy, 2, 1, WIDTH)
+        r_copy(1)
 
-        n = len(GROUPS)
-        for i in range(1, n - 1):
+        last = len(GROUPS) - 1
+        for i in range(1, last):
+            ahead = i + 2
             if i in (2, 4):
-                load_w(i // 2 + 1, 1, 0)
-                load_w(i // 2 + 1, 1, 1)
-            activate(i, 0)
-            activate(i, 1)
-            emit_out(outs.get(i, []))
-            if i + 2 < n:
-                w_interleave_scalar(i + 2)
-            if i + 1 < 8:
-                g_interleave_scalar(i + 1)
-            w_quantize(i + 1)
-            if turned(i - 1):
-                if i >= 2:
-                    h_quantize(i - 2, 0, PAIR)
-                if i + 1 < 8:
-                    w_interleave_vector(i + 2)
-                    g_quantize(i)
-                    g_interleave_vector(i + 1)
-                    g_interleave_gpsimd(i + 1)
-                else:
-                    if i < 8:
-                        g_quantize(i)
-                    w_interleave_vector(i + 2)
-                    w_interleave_gpsimd(i + 2)
-                weigh_turned(i - 1, 0)
-                weigh_turned(i - 1, 1)
-            elif i + 2 < n:
-                h_quantize(i - 2, 0, PAIR)
-                add_direct(i - 1, 0, PAIR)
-                w_interleave_vector(i + 2)
-                weigh_direct(i - 1, 0, PAIR)
-            else:
-                add_direct(i - 1, 0, PAIR)
-                h_quantize(i - 2, 0, PAIR)
-                weigh_direct(i - 1, 0, PAIR)
-            project(i + 1, 0)
-            project(i + 1, 1)
-            emit_passes(passes.get(i, []))
-            if turned(i):
-                turn(i, 0)
-                turn(i, 1)
+                load_w(i // 2 + 1, 1)
 
-        last = n - 1
-        activate(last, 0)
-        activate(last, 1)
-        emit_out([(5, 0), (5, 1), (4, 0), (4, 1)])
+            activate(i)
+            grad_out(nc.scalar.copy, OUTS.get(i, []))
+            if ahead <= last:
+                w_interleave(nc.scalar.copy, ahead, 1, WIDTH)
+            if i + 1 < G_PIECES:
+                interleave(nc.scalar.copy, *g_part(i + 1, G_VECTOR + G_GPSIMD, BANK))
+            if i == 2:
+                nc.scalar.copy(out=c_rows[:], in_=square16(C_ROWS_BANK))
+
+            if i - 1 < TURNED:
+                w_quantize(i + 1)
+                if i >= 2:
+                    h_quantize(i - 2, 0, WIDTH)
+                if ahead < W_HELPED:
+                    w_interleave(nc.vector.tensor_copy, ahead, 0, WIDTH)
+                if i < G_PIECES:
+                    g_quantize(i)
+                if ahead < W_HELPED:
+                    interleave(nc.vector.tensor_copy, *g_part(i + 1, 0, G_VECTOR))
+                    interleave_gpsimd(*g_part(i + 1, G_VECTOR - OVERLAP, G_VECTOR + G_GPSIMD))
+                else:
+                    w_interleave(nc.vector.tensor_copy, ahead, 0, W_VECTOR)
+                    interleave_gpsimd(*w_part(ahead, 0, W_VECTOR - OVERLAP, WIDTH))
+                weigh_turned(i - 1)
+            elif ahead <= last:
+                add_direct(i - 1, 0, WIDTH)
+                w_quantize(i + 1)
+                h_quantize(i - 2, 0, WIDTH)
+                w_interleave(nc.vector.tensor_copy, ahead, 0, W_VECTOR)
+                interleave_gpsimd(*w_part(ahead, 0, W_VECTOR - OVERLAP, WIDTH))
+                weigh_direct(i - 1, 0, WIDTH)
+            else:
+                w_quantize(i + 1)
+                add_direct(i - 1, 0, WIDTH)
+                h_quantize(i - 2, 0, WIDTH)
+                weigh_direct(i - 1, 0, WIDTH)
+
+            project(i + 1)
+            grad_passes(PASSES.get(i, []))
+            if i < TURNED:
+                turn(i)
+            if i == 1:
+                nc.tensor.transpose(square16(C_ROWS_BANK), c_tok[:].rearrange("p j t -> p (j t)"), ident16[:])
+            if i == TURNED:
+                nc.tensor.transpose(square16(C_BANK), c_rows[:], ident16[:])
+
+        activate(last)
+        grad_out(nc.scalar.copy, [(5, 1), (4, 0), (4, 1)])
         add_direct(last - 1, 0, P)
-        h_quantize(last - 2, 0, PAIR)
-        add_direct(last - 1, P, PAIR)
+        h_quantize(last - 2, 0, WIDTH)
+        add_direct(last - 1, P, WIDTH)
         weigh_direct(last - 1, 0, P)
-        weigh_direct(last - 1, P, PAIR)
+        weigh_direct(last - 1, P, WIDTH)
         add_direct(last, 0, P)
-        h_quantize(last - 1, 0, PAIR)
-        emit_passes([(6, vh, 1) for vh in (0, 1)] + [(7, vh, j) for j in (0, 1) for vh in (0, 1)])
-        emit_passes([(6, vh, j) for j in (2, 3) for vh in (0, 1)])
-        emit_out([(6, 0), (6, 1)])
-        add_direct(last, P, PAIR)
+        h_quantize(last - 1, 0, WIDTH)
+        grad_passes([(6, half, 1) for half in (0, 1)] + [(7, half, j) for j in (0, 1) for half in (0, 1)])
+        grad_passes([(6, half, j) for j in (2, 3) for half in (0, 1)])
+        grad_out(nc.scalar.copy, [(6, 0), (6, 1)])
+        add_direct(last, P, WIDTH)
         weigh_direct(last, 0, P)
-        weigh_direct(last, P, PAIR)
+        weigh_direct(last, P, WIDTH)
         h_quantize(last, 0, P)
-        h_quantize(last, P, PAIR)
-        emit_passes([(7, vh, j) for j in (2, 3) for vh in (0, 1)])
-        grad_out(nc.vector.tensor_copy, banks[bank_of[7, 0]], 7, 0)
-        grad_out(nc.scalar.copy, banks[bank_of[7, 1]], 7, 1)
+        h_quantize(last, P, WIDTH)
+        grad_passes([(7, half, j) for j in (2, 3) for half in (0, 1)])
+        grad_out(nc.vector.tensor_copy, [(7, 0)])
+        grad_out(nc.scalar.copy, [(7, 1)])

@@ -28,7 +28,7 @@ TURNED = 8
 TWO_HEADS = 14
 G_PIECES = 2 * HEADS
 
-G_VECTOR, G_GPSIMD = 176, 112
+G_VECTOR, G_GPSIMD = 136, 112
 G_FIRST_VECTOR = 256
 W_HELPED = 9
 W_VECTOR = 144

from contextlib import ExitStack

import concourse.mybir as mybir
from concourse.masks import make_identity

T, HEADS, D, V = 512, 4, 1024, 1024
FLOPS = 2 * T * D * HEADS * D + 2 * HEADS * T * D * V

F32 = mybir.dt.float32
BF16 = mybir.dt.bfloat16
U32 = mybir.dt.uint32
U8 = mybir.dt.uint8
FP8X4 = mybir.dt.float8_e4m3fn_x4
ADD = mybir.AluOpType.add
MULT = mybir.AluOpType.mult
SILU = mybir.ActivationFunctionType.Silu

P = 128
PACK = 4
K_PASS = P * PACK
BANK = 512
WIDTH = 2 * P

GROUPS = ([[(j, 2 * pair), (j, 2 * pair + 1)] for j in range(HEADS) for pair in (0, 1)]
          + [[(j, 4), (j, 5)] for j in range(HEADS)] + [[(j, 6), (j, 7)] for j in (0, 1)]
          + [[(2, tile), (3, tile)] for tile in (6, 7)])
TURNED = 8
TWO_HEADS = 14
G_PIECES = 2 * HEADS

G_VECTOR, G_GPSIMD = 136, 112
G_FIRST_VECTOR = 256
W_HELPED = 9
W_VECTOR = 144
OVERLAP = 4

W_RAW, W_RING, G_RING, H_RING = 6, 3, 2, 2
SILU_TURNED_RING, SILU_DIRECT_RING, DU_RING = 4, 3, 8

Z_BANKS, SUM_BANKS, C_BANK = (0, 1), (2, 3), 2
X_BANKS, R_BANKS, C_ROWS_BANK = (4, 5, 6, 7), (4, 5), 7
DU_BANK = {(0, 0): 4, (0, 1): 5, (1, 0): 6, (1, 1): 7, (2, 0): 3, (3, 0): 4, (2, 1): 6, (3, 1): 5,
           (4, 0): 7, (4, 1): 3, (5, 0): 4, (5, 1): 6, (6, 0): 5, (6, 1): 4, (7, 0): 6, (7, 1): 7}
PASSES = dict([(step, [(tile, step % 2, step // 2 - 1) for tile in (0, 1)]) for step in range(2, 7)] + [
    (8, [(tile, 1, 2) for tile in (0, 1)] + [(tile, 0, 3) for tile in (0, 1)]),
    (9, [(tile, 1, 3) for tile in (0, 1)] + [(tile, 0, j) for tile in (2, 3) for j in range(HEADS)]),
    (10, [(tile, 1, j) for tile in (2, 3) for j in range(HEADS)]),
    (11, [(tile, half, j) for j in (0, 1) for tile, half in ((4, 0), (4, 1), (5, 0))]),
    (12, [(5, 1, j) for j in (0, 1)] + [(tile, half, 2) for tile in (4, 5) for half in (0, 1)]),
    (13, [(tile, half, 3) for tile in (5, 4) for half in (0, 1)]),
    (14, [(6, half, 0) for half in (0, 1)]),
])
OUTS = {9: [(0, 0), (1, 0)], 10: [(0, 1), (1, 1)], 11: [(2, 0), (3, 0)], 12: [(2, 1)], 13: [(3, 1)], 14: [(5, 0)]}


def tile_medusa_unembedding_grad_s7_kernel(tc, x, r, w, c, g, out):
    nc = tc.nc
    with ExitStack() as ctx:
        sb = ctx.enter_context(tc.tile_pool(name="sb", bufs=1))
        ps = ctx.enter_context(tc.psum_pool(name="ps", bufs=1))

        def tiles(name, count, shape, dtype):
            return [sb.tile(shape, dtype, name="%s%d" % (name, i), align_bytes=64) for i in range(count)]

        banks = [ps.tile([P, BANK], F32, name="bank%d" % i) for i in range(8)]
        ident32 = sb.tile([P, P], F32, name="ident32", align_bytes=64)
        ident16 = sb.tile([P, P], BF16, name="ident16", align_bytes=64)
        warm = sb.tile([P, 2], F32, name="warm", align_bytes=64)
        x_raw = tiles("x_raw", PACK, [P, D], BF16)
        r_raw = tiles("r_raw", 2, [P, PACK, BANK], BF16)
        c_tok = sb.tile([P, 8, 16], BF16, name="c_tok", align_bytes=64)
        c_rows = sb.tile([P, P], BF16, name="c_rows", align_bytes=64)
        w_raw = [tiles("w_raw%d_" % i, 2, [P, PACK, BANK], BF16) for i in range(W_RAW)]
        g_raw = tiles("g_raw", HEADS, [P, PACK, V], BF16)
        x_grouped = sb.tile([P, 2, T, PACK], BF16, name="x_grouped", align_bytes=64)
        w_grouped = tiles("w_grouped", W_RING, [P, 2, WIDTH, PACK], BF16)
        g_grouped = tiles("g_grouped", G_RING, [P, BANK, PACK], BF16)
        x_codes = tiles("x_codes", 2, [P, T], U32)
        x_scales = tiles("x_scales", 2, [P, T], U8)
        w_codes = tiles("w_codes", W_RING, [P, 2, WIDTH], U32)
        w_scales = tiles("w_scales", W_RING, [P, 2, WIDTH], U8)
        g_codes = tiles("g_codes", G_PIECES, [P, BANK], U32)
        g_scales = tiles("g_scales", G_PIECES, [P, BANK], U8)
        h_codes = tiles("h_codes", len(GROUPS), [P, WIDTH], U32)
        h_scales = tiles("h_scales", len(GROUPS), [P, WIDTH], U8)
        silu_turned = tiles("silu_turned", SILU_TURNED_RING, [P, T], F32)
        silu_direct = tiles("silu_direct", SILU_DIRECT_RING, [P, WIDTH * PACK], F32)
        h_grouped = tiles("h_grouped", H_RING, [P, WIDTH, PACK], BF16)
        r_turned = tiles("r_turned", 2, [P, 2, T], F32)
        du = tiles("du", DU_RING, [P, BANK], F32)

        def raw_w(j, half):
            return w_raw[(half * HEADS + j) % W_RAW]

        def four_rows(rows):
            return rows.rearrange("(p t) n -> p t n", t=PACK)

        def load_w(j, half):
            cols = slice(j * D + half * BANK, j * D + (half + 1) * BANK)
            for k in range(2):
                nc.sync.dma_start(out=raw_w(j, half)[k][:], in_=four_rows(w[k * K_PASS:(k + 1) * K_PASS, cols]))

        def load_g(j):
            nc.sync.dma_start(out=g_raw[j][:], in_=four_rows(g[j * T:(j + 1) * T, :]))

        def load_r(half):
            nc.sync.dma_start(out=r_raw[half][:], in_=four_rows(r[:, half * BANK:(half + 1) * BANK]))

        def interleave(copy, grouped, raw):
            copy(out=grouped.rearrange("p (n i) t -> p n t i", i=4), in_=raw.rearrange("p t (n i) -> p n t i", i=4))

        def interleave_gpsimd(grouped, raw):
            nc.gpsimd.tensor_scalar(out=grouped, in0=raw.rearrange("p t n -> p n t"), scalar1=1.0, scalar2=0.0, op0=MULT, op1=ADD)

        def quantize(codes, scales, grouped):
            nc.vector.quantize_mx(out=codes.bitcast(FP8X4), scales=scales, in_=grouped)

        def w_part(i, k, lo, hi):
            j, tile = GROUPS[i][lo // P]
            base = tile % 4 * P - lo // P * P
            return w_grouped[i % W_RING][:, k, lo:hi, :], raw_w(j, tile // 4)[k][:, :, base + lo:base + hi]

        def w_interleave(copy, i, k, cols):
            cuts = [0, P, cols] if i >= TWO_HEADS else [0, cols]
            for lo, hi in zip(cuts, cuts[1:]):
                interleave(copy, *w_part(i, k, lo, hi))

        def w_quantize(i):
            quantize(w_codes[i % W_RING][:].rearrange("p k n -> p (k n)"), w_scales[i % W_RING][:].rearrange("p k n -> p (k n)"),
                     w_grouped[i % W_RING][:].rearrange("p k n t -> p (k n t)"))

        def g_part(m, lo, hi):
            j, half = divmod(m, 2)
            return g_grouped[m % G_RING][:, lo:hi, :], g_raw[j][:, :, half * BANK + lo:half * BANK + hi]

        def g_quantize(m):
            quantize(g_codes[m][:], g_scales[m][:], g_grouped[m % G_RING][:].rearrange("p n t -> p (n t)"))

        def x_transpose(t):
            words = x_raw[t][:].bitcast(F32)
            for k in range(2):
                for u in range(2):
                    q = 2 * k + u
                    nc.tensor.transpose(banks[X_BANKS[t]][:, q * P:(q + 1) * P], words[:, 2 * P * k + u:2 * P * (k + 1):2], ident32[:])

        def x_copy(t):
            grouped = x_grouped[:, :, t * P:(t + 1) * P, :].rearrange("p k m t -> p k (m t)").bitcast(F32)
            nc.scalar.copy(out=grouped.rearrange("p k (m u) -> p k m u", u=2),
                           in_=banks[X_BANKS[t]][:].rearrange("p (k u m) -> p k m u", k=2, u=2))

        def x_quantize(k):
            quantize(x_codes[k][:], x_scales[k][:], x_grouped[:, k, :, :].rearrange("p n t -> p (n t)"))

        def r_transpose(pair):
            view = banks[R_BANKS[pair]][:].bitcast(BF16)
            for a in range(2):
                for t in range(PACK):
                    q = a * PACK + t
                    col = pair * WIDTH + a * P
                    nc.tensor.transpose(view[:, q * P:(q + 1) * P], r_raw[0][:, t, col:col + P], ident16[:])

        def r_copy(pair):
            nc.scalar.copy(out=r_turned[pair][:].rearrange("p a n -> p (a n)"), in_=banks[R_BANKS[pair]][:].bitcast(BF16))

        def square16(bank):
            return banks[bank][:].bitcast(BF16)[:, 0:P]

        def mx(acc, lhs_codes, lhs_scales, rhs_codes, rhs_scales, start, stop):
            nc.tensor.matmul_mx(out=acc, lhsT=lhs_codes.bitcast(FP8X4), lhsT_scale=lhs_scales,
                                rhs=rhs_codes.bitcast(FP8X4), rhs_scale=rhs_scales, start=start, stop=stop)

        def project(i):
            codes, scales = w_codes[i % W_RING], w_scales[i % W_RING]
            for a in range(2):
                bank = banks[Z_BANKS[a]]
                if i < TURNED:
                    cols = slice(a * P, (a + 1) * P)
                    for k in range(2):
                        mx(bank[:], codes[:, k, cols], scales[:, k, cols], x_codes[k][:], x_scales[k][:], k == 0, k == 1)
                else:
                    for e in range(2):
                        cols = slice((2 * a + e) * P, (2 * a + e + 1) * P)
                        for k in range(2):
                            mx(bank[:, e * WIDTH:(e + 1) * WIDTH], x_codes[k][:, cols], x_scales[k][:, cols],
                               codes[:, k, :], scales[:, k, :], k == 0, k == 1)

        def activate(i):
            for a in range(2):
                bank = banks[Z_BANKS[a]]
                if i < TURNED:
                    nc.scalar.activation(out=silu_turned[(2 * i + a) % SILU_TURNED_RING][:], in_=bank[:], func=SILU)
                else:
                    heads = 2 if i >= TWO_HEADS else 1
                    parts = silu_direct[i % SILU_DIRECT_RING][:].rearrange("p (b a n e) -> p b a n e", b=heads, a=2, e=2)
                    nc.scalar.activation(out=parts[:, :, a, :, :], in_=bank[:].rearrange("p (e b n) -> p b n e", e=2, b=heads), func=SILU)

        def turn(i):
            for a in range(2):
                tile = GROUPS[i][a][1]
                for t in range(PACK):
                    cols = slice(t * P, (t + 1) * P)
                    acc = banks[SUM_BANKS[a]][:, cols]
                    nc.tensor.matmul(acc, lhsT=r_turned[tile // 2][:, tile % 2, cols], rhs=ident32[:],
                                     start=True, stop=False, is_transpose=True)
                    nc.tensor.matmul(acc, lhsT=silu_turned[(2 * i + a) % SILU_TURNED_RING][:, cols], rhs=ident32[:],
                                     start=False, stop=True, is_transpose=True)

        def c_spread(table, j, n):
            return table[:, j, 0:PACK].unsqueeze(1).to_broadcast([P, n, PACK])

        def weigh_turned(i):
            for a in range(2):
                nc.vector.tensor_tensor(out=h_grouped[i % H_RING][:, a * P:(a + 1) * P, :],
                                        in0=banks[SUM_BANKS[a]][:].rearrange("p (t n) -> p n t", t=PACK),
                                        in1=c_spread(c_tok[:], GROUPS[i][a][0], P), op=MULT)

        def silu_part(i, lo, hi):
            return silu_direct[i % SILU_DIRECT_RING][:, lo * PACK:hi * PACK].rearrange("p (a n e) -> p a n e", a=2, e=2)

        def add_direct(i, lo, hi):
            base = GROUPS[i][lo // P][1] % 4 * P - lo // P * P
            nc.vector.tensor_tensor(out=silu_part(i, lo, hi), in0=silu_part(i, lo, hi),
                                    in1=r_raw[1][:, :, base + lo:base + hi].rearrange("p (a e) n -> p a n e", e=2), op=ADD)

        def weigh_direct(i, lo, hi):
            table = square16(C_BANK).rearrange("p (j t) -> p j t", t=16)
            nc.vector.tensor_tensor(out=h_grouped[i % H_RING][:, lo:hi, :].rearrange("p n (a e) -> p n a e", e=2),
                                    in0=silu_part(i, lo, hi).rearrange("p a n e -> p n a e"),
                                    in1=c_spread(table, GROUPS[i][lo // P][0], hi - lo).rearrange("p n (a e) -> p n a e", e=2), op=MULT)

        def h_quantize(i, lo, hi):
            quantize(h_codes[i][:, lo:hi], h_scales[i][:, lo:hi], h_grouped[i % H_RING][:, lo:hi, :].rearrange("p n t -> p (n t)"))

        place = {unit: (i, a) for i, units in enumerate(GROUPS) for a, unit in enumerate(units)}
        stored = []

        def grad_passes(todo):
            for tile, half, j in todo:
                i, a = place[j, tile]
                cols = slice(a * P, (a + 1) * P)
                mx(banks[DU_BANK[tile, half]][:], h_codes[i][:, cols], h_scales[i][:, cols],
                   g_codes[2 * j + half][:], g_scales[2 * j + half][:], j == 0, j == HEADS - 1)

        def grad_out(copy, todo):
            for tile, half in todo:
                stage = du[len(stored) % DU_RING]
                stored.append((tile, half))
                copy(out=stage[:], in_=banks[DU_BANK[tile, half]][:])
                nc.sync.dma_start(out=out[tile * P:(tile + 1) * P, half * BANK:(half + 1) * BANK], in_=stage[:])

        ctx.enter_context(tc.manual_schedule())

        nc.vector.memset(c_tok[:], 0.0)
        for t in range(PACK):
            nc.sync.dma_start(out=x_raw[t][:], in_=four_rows(x)[:, t, :])
        load_w(0, 0)
        load_g(0)
        load_r(0)
        nc.sync.dma_start(out=c_tok[:, 0:HEADS, 0:PACK], in_=c.rearrange("j (p t) -> p j t", t=PACK))
        for j in range(1, HEADS):
            load_w(j, 0)
            load_g(j)
        load_r(1)
        for j in range(W_RAW - HEADS):
            load_w(j, 1)

        make_identity(nc, ident32[:])
        make_identity(nc, ident16[:])
        nc.vector.memset(warm[:], 0.0)
        nc.scalar.activation(out=warm[:, 1:2], in_=warm[:, 0:1], func=SILU)

        for t in range(PACK):
            x_transpose(t)
        for t in range(PACK):
            x_copy(t)
        w_interleave(nc.vector.tensor_copy, 0, 0, WIDTH)
        w_interleave(nc.vector.tensor_copy, 1, 0, WIDTH)
        w_interleave(nc.vector.tensor_copy, 0, 1, WIDTH)
        w_interleave(nc.scalar.copy, 1, 1, WIDTH)
        x_quantize(0)
        w_quantize(0)
        x_quantize(1)
        project(0)
        interleave(nc.scalar.copy, *g_part(0, G_FIRST_VECTOR, BANK))
        w_quantize(1)
        interleave(nc.vector.tensor_copy, *g_part(0, 0, G_FIRST_VECTOR))
        r_transpose(0)
        r_transpose(1)
        activate(0)
        r_copy(0)
        interleave(nc.vector.tensor_copy, *g_part(1, 0, BANK))
        g_quantize(0)
        project(1)
        turn(0)
        w_interleave(nc.vector.tensor_copy, 2, 0, WIDTH)
        w_interleave(nc.vector.tensor_copy, 2, 1, WIDTH)
        r_copy(1)

        last = len(GROUPS) - 1
        for i in range(1, last):
            ahead = i + 2
            if i in (2, 4):
                load_w(i // 2 + 1, 1)

            activate(i)
            grad_out(nc.scalar.copy, OUTS.get(i, []))
            if ahead <= last:
                w_interleave(nc.scalar.copy, ahead, 1, WIDTH)
            if i + 1 < G_PIECES:
                interleave(nc.scalar.copy, *g_part(i + 1, G_VECTOR + G_GPSIMD, BANK))
            if i == 2:
                nc.scalar.copy(out=c_rows[:], in_=square16(C_ROWS_BANK))

            if i - 1 < TURNED:
                w_quantize(i + 1)
                if i >= 2:
                    h_quantize(i - 2, 0, WIDTH)
                if ahead < W_HELPED:
                    w_interleave(nc.vector.tensor_copy, ahead, 0, WIDTH)
                if i < G_PIECES:
                    g_quantize(i)
                if ahead < W_HELPED:
                    interleave(nc.vector.tensor_copy, *g_part(i + 1, 0, G_VECTOR))
                    interleave_gpsimd(*g_part(i + 1, G_VECTOR - OVERLAP, G_VECTOR + G_GPSIMD))
                else:
                    w_interleave(nc.vector.tensor_copy, ahead, 0, W_VECTOR)
                    interleave_gpsimd(*w_part(ahead, 0, W_VECTOR - OVERLAP, WIDTH))
                weigh_turned(i - 1)
            elif ahead <= last:
                add_direct(i - 1, 0, WIDTH)
                w_quantize(i + 1)
                h_quantize(i - 2, 0, WIDTH)
                w_interleave(nc.vector.tensor_copy, ahead, 0, W_VECTOR)
                interleave_gpsimd(*w_part(ahead, 0, W_VECTOR - OVERLAP, WIDTH))
                weigh_direct(i - 1, 0, WIDTH)
            else:
                w_quantize(i + 1)
                add_direct(i - 1, 0, WIDTH)
                h_quantize(i - 2, 0, WIDTH)
                weigh_direct(i - 1, 0, WIDTH)

            project(i + 1)
            grad_passes(PASSES.get(i, []))
            if i < TURNED:
                turn(i)
            if i == 1:
                nc.tensor.transpose(square16(C_ROWS_BANK), c_tok[:].rearrange("p j t -> p (j t)"), ident16[:])
            if i == TURNED:
                nc.tensor.transpose(square16(C_BANK), c_rows[:], ident16[:])

        activate(last)
        grad_out(nc.scalar.copy, [(5, 1), (4, 0), (4, 1)])
        add_direct(last - 1, 0, P)
        h_quantize(last - 2, 0, WIDTH)
        add_direct(last - 1, P, WIDTH)
        weigh_direct(last - 1, 0, P)
        weigh_direct(last - 1, P, WIDTH)
        add_direct(last, 0, P)
        h_quantize(last - 1, 0, WIDTH)
        grad_passes([(6, half, 1) for half in (0, 1)] + [(7, half, j) for j in (0, 1) for half in (0, 1)])
        grad_passes([(6, half, j) for j in (2, 3) for half in (0, 1)])
        grad_out(nc.scalar.copy, [(6, 0), (6, 1)])
        add_direct(last, P, WIDTH)
        weigh_direct(last, 0, P)
        weigh_direct(last, P, WIDTH)
        h_quantize(last, 0, P)
        h_quantize(last, P, WIDTH)
        grad_passes([(7, half, j) for j in (2, 3) for half in (0, 1)])
        grad_out(nc.vector.tensor_copy, [(7, 0)])
        grad_out(nc.scalar.copy, [(7, 1)])
